import numpy as np
import ml_dtypes


def mxq(x, axis, fmt="e4m3"):
    dtype, down = {"e4m3": (ml_dtypes.float8_e4m3fn, 7), "e5m2": (ml_dtypes.float8_e5m2, 14)}[fmt]
    v = np.moveaxis(np.asarray(x, np.float32).astype(ml_dtypes.bfloat16).astype(np.float64), axis, -1)
    blocks = v.reshape(v.shape[:-1] + (-1, 32))
    amax = np.abs(blocks).max(-1, keepdims=True)
    byte = np.maximum(np.where(amax > 0, np.frexp(amax)[1] - 1 + 127, 0) - down, 1)
    scale = np.exp2(byte - 127.0)
    codes = (blocks / scale).astype(np.float32).astype(dtype).astype(np.float64)
    return np.moveaxis((codes * scale).reshape(v.shape), -1, axis)


WIDE = False


def mx_kscale(k):
    if not WIDE:
        return np.ones(k)
    levels = np.array([10, -10, 5, -5, 0])
    if k % 512:
        return np.exp2(np.random.permutation(np.resize(levels, k // 32))).repeat(32)
    a = np.empty((k // 512, 16))
    for p in range(k // 512):
        a[p, :8] = np.random.permutation(np.resize(levels, 8))
        for g in range(8):
            far = levels[np.abs(levels - a[p, g]) >= 10]
            a[p, g + 8] = far[np.random.randint(len(far))]
    return np.exp2(a.ravel()).repeat(32)


def f64(x):
    return np.asarray(x).astype(np.float64)


def striped(idx):
    return np.tile(idx.reshape(-1, 16).T, (8, 1)).astype(np.uint16)


def unstriped(offs):
    return offs[:16].T.reshape(-1).astype(np.int64)


def gelu(v):
    return 0.5 * v * (1.0 + np.tanh(np.sqrt(2.0 / np.pi) * (v + 0.044715 * v**3)))


K, T, E, C, H, N = 1536, 512, 4, 256, 512, 128


def by_expert(wq, xq):
    return np.concatenate([wq[e].T @ xq[:, e * C:(e + 1) * C] for e in range(E)], axis=1)


def setup_inputs():
    n = np.random.standard_normal
    s = mx_kscale(K)[:, None]
    u = mx_kscale(H)
    first = np.random.permutation(np.repeat(np.arange(E), T // E))
    second = (first + 1 + np.random.permutation(np.repeat(np.arange(E - 1), -(-T // (E - 1)))[:T])) % E
    while np.bincount(second, minlength=E).max() != T // E:
        load = np.bincount(second, minlength=E); hi, lo = int(load.argmax()), int(load.argmin())
        t = np.flatnonzero((second == hi) & (first != lo))[0]; second[t] = lo
    slot_token = np.empty(E * C, np.int64); pos = np.empty((2, T), np.int64); fill = np.zeros(E, np.int64)
    place = np.stack([np.random.permutation(C) for _ in range(E)])
    for r, deal in enumerate((first, second)):
        for t in np.random.permutation(T):
            e = deal[t]; j = e * C + place[e, fill[e]]; fill[e] += 1; slot_token[j] = t; pos[r, t] = j
    g = np.random.uniform(0.2, 0.8, T)
    return {
        "xT": (n((K, T)) * s).astype(np.float32),
        "w1": (n((E, K, H)) / np.sqrt(K) / s[None] * u[None, None, :]).astype(np.float32),
        "w2": (n((E, H, N)) / np.sqrt(H) / u[None, :, None]).astype(np.float32),
        "gate": np.stack([np.tile(g, (N, 1)), np.tile(1.0 - g, (N, 1))]).astype(np.float32),
        "offs": striped(slot_token),
        "pos1": striped(pos[0]),
        "pos2": striped(pos[1]),
    }


def reference(xT, w1, w2, gate, offs, pos1, pos2):
    idx = unstriped(offs)
    xq = mxq(f64(xT)[:, idx], 0, "e4m3")
    h = gelu(by_expert(mxq(f64(w1), 1, "e4m3"), xq))
    y = by_expert(mxq(f64(w2), 1, "e4m3"), mxq(h, 0, "e4m3"))
    return f64(gate[0]) * y[:, unstriped(pos1)] + f64(gate[1]) * y[:, unstriped(pos2)]

@@ -1,0 +1,259 @@
+from contextlib import ExitStack
+
+import concourse.mybir as mybir
+
+K, T, E, C, H, N = 1536, 512, 4, 256, 512, 128
+FLOPS = 2 * E * C * H * (K + N)
+
+F32 = mybir.dt.float32
+BF16 = mybir.dt.bfloat16
+U32 = mybir.dt.uint32
+U16 = mybir.dt.uint16
+U8 = mybir.dt.uint8
+FP8X4 = mybir.dt.float8_e4m3fn_x4
+
+MULT = mybir.AluOpType.mult
+ADD = mybir.AluOpType.add
+GELU = mybir.ActivationFunctionType.Gelu_apprx_tanh
+
+P = 128
+PACK = 4
+K_PASS = P * PACK
+PASSES = K // K_PASS
+PIECES = E * PASSES
+SLOTS = E * C
+HALF = C // 2
+TILES = H // P
+LINE = 4
+LIST_ROWS = 16
+
+SCALE_ROWS = 4
+SLOT_CUTS = [0, 384, 768, 1024]
+LATE_EXPERTS = 2
+
+VECTOR_TOKENS = [256, 64, 64]
+VECTOR_GROUPS = [0, 0, 0, 72, 72, 72, 72, 96, 96, 72, 72, 80]
+
+RAW_PLACES = 8
+RAW_BYTES = PACK * H * 4
+GELU_OVER = [[5, 6], [6, 7], [11, 11]]
+LAST_PARTS = 4
+
+
+def place_of(q):
+    return q % RAW_PLACES * RAW_BYTES
+
+
+def shared_copy(nc, dst, src, cut):
+    if cut > 0:
+        nc.vector.tensor_copy(dst[:, :cut], src[:, :cut])
+    if cut < dst.shape[1]:
+        nc.scalar.copy(dst[:, cut:], src[:, cut:])
+
+
+def tile_routed_moe_kernel(tc, xT, w1, w2, gate, offs, pos1, pos2, out):
+    nc = tc.nc
+    with ExitStack() as ctx:
+        keep = ctx.enter_context(tc.tile_pool(name="keep", bufs=1))
+        token_groups = ctx.enter_context(tc.tile_pool(name="token_groups", bufs=PASSES))
+        raws = ctx.enter_context(tc.tile_pool(name="raws", bufs=1))
+        w1_groups = ctx.enter_context(tc.tile_pool(name="w1_groups", bufs=5))
+        hidden = ctx.enter_context(tc.tile_pool(name="hidden", bufs=4))
+        psum_h = ctx.enter_context(tc.psum_pool(name="psum_h", bufs=5))
+        psum_y = ctx.enter_context(tc.psum_pool(name="psum_y", bufs=3))
+
+        offs_list = keep.tile([P, SLOTS // LIST_ROWS], U16, name="offs_list")
+        pos1_list = keep.tile([P, T // LIST_ROWS], U16, name="pos1_list")
+        pos2_list = keep.tile([P, T // LIST_ROWS], U16, name="pos2_list")
+        gate_rows = keep.tile([P, 2, T], F32, name="gate_rows")
+
+        token_scales = keep.tile([P, T], U8, name="token_scales", align_bytes=64)
+        nc.gpsimd.memset(token_scales[:], 0)
+
+        x_raw = []
+        for g in range(PASSES):
+            raw = keep.tile([P, PACK, T], F32, name=f"x_raw{g}")
+            nc.sync.dma_start(raw[:], xT[g * K_PASS : (g + 1) * K_PASS, :].rearrange("(p j) t -> p j t", j=PACK))
+            x_raw.append(raw)
+            if g == 0:
+                nc.sync.dma_start(offs_list[:], offs)
+
+        w1_raw = {}
+
+        def load_w1(q):
+            e, g = q // PASSES, q % PASSES
+            raw = raws.tile([P, PACK, H], F32, name=f"w1_raw{q}", offset=place_of(q), align_bytes=64)
+            src = w1[e, g * K_PASS : (g + 1) * K_PASS, :].rearrange("(p j) c -> p j c", j=PACK)
+            nc.sync.dma_start(raw[:], src)
+            w1_raw[q] = raw
+
+        w2_raw = keep.tile([P, E, PACK, N], F32, name="w2_raw")
+        w2_rows = w2.rearrange("e (p j) n -> p e j n", j=PACK)
+
+        for q in range(PASSES):
+            load_w1(q)
+        nc.sync.dma_start(w2_raw[:, : E - LATE_EXPERTS], w2_rows[:, : E - LATE_EXPERTS])
+        for q in range(PASSES, RAW_PLACES):
+            load_w1(q)
+
+        token_codes = []
+        for g in range(PASSES):
+            grouped = token_groups.tile([P, T, PACK], BF16, name="grouped", align_bytes=64)
+            shared_copy(
+                nc,
+                grouped[:].rearrange("p (c i) j -> p c j i", i=LINE),
+                x_raw[g][:].rearrange("p j (c i) -> p c j i", i=LINE),
+                VECTOR_TOKENS[g] // LINE,
+            )
+            codes = keep.tile([P, T], U32, name=f"token_codes{g}", align_bytes=64)
+            nc.vector.quantize_mx(
+                out=codes[:].bitcast(FP8X4),
+                scales=token_scales[SCALE_ROWS * g : P, :],
+                in_=grouped[:].rearrange("p t j -> p (t j)"),
+            )
+            token_codes.append(codes)
+
+        slot_codes = keep.tile([P, PASSES, SLOTS], U32, name="slot_codes", align_bytes=64)
+        slot_scales = keep.tile([P, SLOTS], U8, name="slot_scales", align_bytes=64)
+        for a, b in zip(SLOT_CUTS[:-1], SLOT_CUTS[1:]):
+            entries = offs_list[:, a // LIST_ROWS : b // LIST_ROWS]
+            for g in range(PASSES):
+                nc.vector.tensor_copy(slot_codes[:, g, a:b], token_codes[g][:].indirect(entries))
+            nc.vector.tensor_copy(slot_scales[:, a:b], token_scales[:].indirect(entries))
+
+        w1_grouped = {}
+        w1_codes = {}
+        w1_scales = {}
+
+        def interleave(q):
+            grouped = w1_groups.tile([P, H * PACK], BF16, name="w1_grouped", align_bytes=64)
+            dst = grouped[:].rearrange("p (t m j) -> p m j t", t=TILES, j=PACK)
+            src = w1_raw[q][:].rearrange("p j (m t) -> p m j t", t=TILES)
+            shared_copy(nc, dst, src, VECTOR_GROUPS[q])
+            w1_grouped[q] = grouped
+
+        def quantise(q):
+            codes = keep.tile([P, H], U32, name=f"w1_codes{q}", align_bytes=64)
+            scales = keep.tile([P, H], U8, name=f"w1_scales{q}", align_bytes=64)
+            parts = LAST_PARTS if q == PIECES - 1 else 1
+            width = H // parts
+            for i in range(parts):
+                cols = slice(i * width, (i + 1) * width)
+                nc.vector.quantize_mx(
+                    out=codes[:, cols].bitcast(FP8X4),
+                    scales=scales[:, cols],
+                    in_=w1_grouped[q][:, i * width * PACK : (i + 1) * width * PACK],
+                )
+            w1_codes[q] = codes
+            w1_scales[q] = scales
+
+        w2_grouped = keep.tile([P, E, N, PACK], BF16, name="w2_grouped", align_bytes=64)
+        w2_codes = keep.tile([P, E * N], U32, name="w2_codes", align_bytes=64)
+        w2_scales = keep.tile([P, E * N], U8, name="w2_scales", align_bytes=64)
+
+        def second_weights(first, last, copy):
+            for e in range(first, last):
+                copy(
+                    w2_grouped[:, e].rearrange("p (c i) j -> p c j i", i=LINE),
+                    w2_raw[:, e].rearrange("p j (c i) -> p c j i", i=LINE),
+                )
+            cols = slice(first * N, last * N)
+            nc.vector.quantize_mx(
+                out=w2_codes[:, cols].bitcast(FP8X4),
+                scales=w2_scales[:, cols],
+                in_=w2_grouped[:, first:last].rearrange("p e n j -> p (e n j)"),
+            )
+
+        hidden_sums = {}
+
+        def first_layer(e):
+            for b in range(2):
+                cols = slice(e * C + b * HALF, e * C + (b + 1) * HALF)
+                sums = psum_h.tile([P, TILES, HALF], F32, name="hidden_sums")
+                for t in range(TILES):
+                    channels = slice(t * P, (t + 1) * P)
+                    for g in range(PASSES):
+                        q = e * PASSES + g
+                        nc.tensor.matmul_mx(
+                            out=sums[:, t, :],
+                            lhsT=w1_codes[q][:, channels].bitcast(FP8X4),
+                            lhsT_scale=w1_scales[q][:, channels],
+                            rhs=slot_codes[:, g, cols].bitcast(FP8X4),
+                            rhs_scale=slot_scales[SCALE_ROWS * g : P, cols],
+                            start=(g == 0),
+                            stop=(g == PASSES - 1),
+                        )
+                hidden_sums[(e, b)] = sums
+
+        y_sums = {}
+
+        def second_layer(e, b):
+            if e < E - 1:
+                place = place_of(GELU_OVER[e][b]) + b * HALF * PACK * 2
+                h = raws.tile([P, HALF * PACK], BF16, name=f"h{e}_{b}", offset=place, align_bytes=64)
+            else:
+                h = hidden.tile([P, HALF * PACK], BF16, name="h_last", align_bytes=64)
+            nc.scalar.activation(
+                h[:].rearrange("p (s t) -> p s t", t=TILES), hidden_sums[(e, b)][:].rearrange("p t s -> p s t"), GELU
+            )
+            codes = hidden.tile([P, HALF], U32, name="h_codes", align_bytes=64)
+            scales = hidden.tile([P, HALF], U8, name="h_scales", align_bytes=64)
+            nc.vector.quantize_mx(out=codes[:].bitcast(FP8X4), scales=scales[:], in_=h[:])
+            if b == 0 or e == E - 1:
+                sums = psum_y.tile([P, C], F32, name="y_sums")
+                y_sums[(e, b)] = sums
+            else:
+                y_sums[(e, b)] = y_sums[(e, 0)]
+            channels = slice(e * N, (e + 1) * N)
+            nc.tensor.matmul_mx(
+                out=y_sums[(e, b)][:, b * HALF : (b + 1) * HALF],
+                lhsT=w2_codes[:, channels].bitcast(FP8X4),
+                lhsT_scale=w2_scales[:, channels],
+                rhs=codes[:].bitcast(FP8X4),
+                rhs_scale=scales[:],
+                start=True,
+                stop=True,
+            )
+
+        y_slots = keep.tile([P, SLOTS], F32, name="y_slots")
+
+        for q in range(PIECES):
+            interleave(q)
+            if q + RAW_PLACES < PIECES:
+                load_w1(q + RAW_PLACES)
+            elif q + RAW_PLACES == PIECES:
+                nc.sync.dma_start(w2_raw[:, E - LATE_EXPERTS :], w2_rows[:, E - LATE_EXPERTS :])
+                nc.sync.dma_start(pos1_list[:], pos1)
+                nc.sync.dma_start(pos2_list[:], pos2)
+                nc.sync.dma_start(gate_rows[:], gate.rearrange("r n t -> n r t"))
+            quantise(q)
+            if q == PASSES - 1:
+                second_weights(0, E - LATE_EXPERTS, nc.scalar.copy)
+            if q == PIECES - 1:
+                second_weights(E - LATE_EXPERTS, E, nc.vector.tensor_copy)
+            if q % PASSES == PASSES - 1:
+                first_layer(q // PASSES)
+            for e in range(E - 1):
+                for b in range(2):
+                    if q == GELU_OVER[e][b]:
+                        second_layer(e, b)
+                        if b == 1:
+                            nc.scalar.copy(y_slots[:, e * C : (e + 1) * C], y_sums[(e, 0)][:])
+        for b in range(2):
+            second_layer(E - 1, b)
+        for b, copy in ((0, nc.vector.tensor_copy), (1, nc.scalar.copy)):
+            cols = slice((E - 1) * C + b * HALF, (E - 1) * C + (b + 1) * HALF)
+            copy(y_slots[:, cols], y_sums[(E - 1, b)][:, b * HALF : (b + 1) * HALF])
+
+        first = keep.tile([P, T], F32, name="first")
+        nc.vector.tensor_tensor(first[:], y_slots[:].indirect(pos1_list[:]), gate_rows[:, 0, :], MULT)
+        width = T // 2
+        token_halves = [slice(i * width, (i + 1) * width) for i in range(2)]
+        second = keep.tile([P, T], F32, name="second")
+        for tokens in token_halves:
+            entries = pos2_list[:, tokens.start // LIST_ROWS : tokens.stop // LIST_ROWS]
+            nc.vector.tensor_tensor(second[:, tokens], y_slots[:].indirect(entries), gate_rows[:, 1, tokens], MULT)
+        for tokens in token_halves:
+            total = hidden.tile([P, width], F32, name="total")
+            nc.vector.tensor_tensor(total[:], first[:, tokens], second[:, tokens], ADD)
+            nc.sync.dma_start(out[:, tokens], total[:])

@@ -7,6 +7,7 @@ FLOPS = 2 * E * C * H * (K + N)
 
 F32 = mybir.dt.float32
 BF16 = mybir.dt.bfloat16
+I32 = mybir.dt.int32
 U32 = mybir.dt.uint32
 U16 = mybir.dt.uint16
 U8 = mybir.dt.uint8
@@ -28,20 +29,22 @@ LINE = 4
 LIST_ROWS = 16
 
 SCALE_ROWS = 4
-SLOT_CUTS = [0, 384, 768, 1024]
-LATE_EXPERTS = 2
+WINDOW = 1408
 
-VECTOR_TOKENS = [256, 64, 64]
-VECTOR_GROUPS = [0, 0, 0, 72, 72, 72, 72, 96, 96, 72, 72, 80]
+VECTOR_TOKENS = [320, 64, 64]
+VECTOR_GROUPS = [0, 0, 0, 0, 96, 64, 56, 88, 76, 76, 76]
 
-RAW_PLACES = 8
 RAW_BYTES = PACK * H * 4
-GELU_OVER = [[5, 6], [6, 7], [11, 11]]
-LAST_PARTS = 4
+RAW_PLACES = 11
+W2_PLACE = RAW_PLACES * RAW_BYTES
+W2_BYTES = PACK * N * 4
+LAST_CODES_PLACE = W2_PLACE + E * W2_BYTES
+GELU_OVER = [3, 6, 9]
+LAST_CUTS = [0, 256, 384, 512]
 
 
 def place_of(q):
-    return q % RAW_PLACES * RAW_BYTES
+    return (PASSES + q) % RAW_PLACES * RAW_BYTES
 
 
 def shared_copy(nc, dst, src, cut):
@@ -58,27 +61,30 @@ def tile_routed_moe_kernel(tc, xT, w1, w2, gate, offs, pos1, pos2, out):
         token_groups = ctx.enter_context(tc.tile_pool(name="token_groups", bufs=PASSES))
         raws = ctx.enter_context(tc.tile_pool(name="raws", bufs=1))
         w1_groups = ctx.enter_context(tc.tile_pool(name="w1_groups", bufs=5))
-        hidden = ctx.enter_context(tc.tile_pool(name="hidden", bufs=4))
-        psum_h = ctx.enter_context(tc.psum_pool(name="psum_h", bufs=5))
-        psum_y = ctx.enter_context(tc.psum_pool(name="psum_y", bufs=3))
+        psum_h = ctx.enter_context(tc.psum_pool(name="psum_h", bufs=4))
+        psum_y = ctx.enter_context(tc.psum_pool(name="psum_y", bufs=1))
 
         offs_list = keep.tile([P, SLOTS // LIST_ROWS], U16, name="offs_list")
         pos1_list = keep.tile([P, T // LIST_ROWS], U16, name="pos1_list")
         pos2_list = keep.tile([P, T // LIST_ROWS], U16, name="pos2_list")
         gate_rows = keep.tile([P, 2, T], F32, name="gate_rows")
 
-        token_scales = keep.tile([P, T], U8, name="token_scales", align_bytes=64)
+        token_codes = keep.tile([P, PASSES, WINDOW], U32, name="token_codes", align_bytes=64)
+        nc.vector.memset(token_codes[:, :, T:].bitcast(I32), 0)
+        token_scales = keep.tile([P, WINDOW], U8, name="token_scales", align_bytes=64)
         nc.gpsimd.memset(token_scales[:], 0)
 
+        warm = keep.tile([P, 2], F32, name="warm")
+        nc.vector.memset(warm[:, :1], 0.0)
+        nc.scalar.activation(warm[:, 1:], warm[:, :1], GELU)
+
         x_raw = []
-        for g in range(PASSES):
-            raw = keep.tile([P, PACK, T], F32, name=f"x_raw{g}")
+        w1_raw = {}
+
+        def load_x(g):
+            raw = raws.tile([P, PACK, T], F32, name=f"x_raw{g}", offset=g * RAW_BYTES, align_bytes=64)
             nc.sync.dma_start(raw[:], xT[g * K_PASS : (g + 1) * K_PASS, :].rearrange("(p j) t -> p j t", j=PACK))
             x_raw.append(raw)
-            if g == 0:
-                nc.sync.dma_start(offs_list[:], offs)
-
-        w1_raw = {}
 
         def load_w1(q):
             e, g = q // PASSES, q % PASSES
@@ -87,16 +93,21 @@ def tile_routed_moe_kernel(tc, xT, w1, w2, gate, offs, pos1, pos2, out):
             nc.sync.dma_start(raw[:], src)
             w1_raw[q] = raw
 
-        w2_raw = keep.tile([P, E, PACK, N], F32, name="w2_raw")
-        w2_rows = w2.rearrange("e (p j) n -> p e j n", j=PACK)
-
-        for q in range(PASSES):
+        load_x(0)
+        nc.sync.dma_start(offs_list[:], offs)
+        load_x(1)
+        load_w1(0)
+        load_x(2)
+        for q in range(1, RAW_PLACES - PASSES):
             load_w1(q)
-        nc.sync.dma_start(w2_raw[:, : E - LATE_EXPERTS], w2_rows[:, : E - LATE_EXPERTS])
-        for q in range(PASSES, RAW_PLACES):
-            load_w1(q)
 
-        token_codes = []
+        slot_codes = {}
+
+        def gather_codes(g, codes):
+            nc.vector.tensor_copy(codes[:], token_codes[:, g, :].indirect(offs_list[:]))
+            slot_codes[g] = codes
+
+        slot_scales = keep.tile([P, SLOTS], U8, name="slot_scales", align_bytes=64)
         for g in range(PASSES):
             grouped = token_groups.tile([P, T, PACK], BF16, name="grouped", align_bytes=64)
             shared_copy(
@@ -105,155 +116,177 @@ def tile_routed_moe_kernel(tc, xT, w1, w2, gate, offs, pos1, pos2, out):
                 x_raw[g][:].rearrange("p j (c i) -> p c j i", i=LINE),
                 VECTOR_TOKENS[g] // LINE,
             )
-            codes = keep.tile([P, T], U32, name=f"token_codes{g}", align_bytes=64)
             nc.vector.quantize_mx(
-                out=codes[:].bitcast(FP8X4),
-                scales=token_scales[SCALE_ROWS * g : P, :],
+                out=token_codes[:, g, :T].bitcast(FP8X4),
+                scales=token_scales[SCALE_ROWS * g : P, :T],
                 in_=grouped[:].rearrange("p t j -> p (t j)"),
             )
-            token_codes.append(codes)
-
-        slot_codes = keep.tile([P, PASSES, SLOTS], U32, name="slot_codes", align_bytes=64)
-        slot_scales = keep.tile([P, SLOTS], U8, name="slot_scales", align_bytes=64)
-        for a, b in zip(SLOT_CUTS[:-1], SLOT_CUTS[1:]):
-            entries = offs_list[:, a // LIST_ROWS : b // LIST_ROWS]
-            for g in range(PASSES):
-                nc.vector.tensor_copy(slot_codes[:, g, a:b], token_codes[g][:].indirect(entries))
-            nc.vector.tensor_copy(slot_scales[:, a:b], token_scales[:].indirect(entries))
+            if g < PASSES - 1:
+                gather_codes(g, keep.tile([P, SLOTS], U32, name=f"slot_codes{g}", align_bytes=64))
+            load_w1(RAW_PLACES - PASSES + g)
+        nc.vector.tensor_copy(slot_scales[:], token_scales[:].indirect(offs_list[:]))
 
         w1_grouped = {}
         w1_codes = {}
         w1_scales = {}
 
         def interleave(q):
-            grouped = w1_groups.tile([P, H * PACK], BF16, name="w1_grouped", align_bytes=64)
+            if q == 1:
+                grouped = raws.tile([P, H * PACK], BF16, name="w1_grouped1", offset=LAST_CODES_PLACE, align_bytes=64)
+            else:
+                grouped = w1_groups.tile([P, H * PACK], BF16, name="w1_grouped", align_bytes=64)
             dst = grouped[:].rearrange("p (t m j) -> p m j t", t=TILES, j=PACK)
             src = w1_raw[q][:].rearrange("p j (m t) -> p m j t", t=TILES)
-            shared_copy(nc, dst, src, VECTOR_GROUPS[q])
+            if q < PIECES - 1:
+                shared_copy(nc, dst, src, VECTOR_GROUPS[q])
+            else:
+                nc.vector.tensor_copy(dst[:, :, :, :2], src[:, :, :, :2])
+                nc.scalar.copy(dst[:, :, :, 2:], src[:, :, :, 2:])
             w1_grouped[q] = grouped
 
         def quantise(q):
             codes = keep.tile([P, H], U32, name=f"w1_codes{q}", align_bytes=64)
             scales = keep.tile([P, H], U8, name=f"w1_scales{q}", align_bytes=64)
-            parts = LAST_PARTS if q == PIECES - 1 else 1
-            width = H // parts
-            for i in range(parts):
-                cols = slice(i * width, (i + 1) * width)
+            cuts = LAST_CUTS if q == PIECES - 1 else [0, H]
+            for a, b in zip(cuts[:-1], cuts[1:]):
+                cols = slice(a, b)
                 nc.vector.quantize_mx(
                     out=codes[:, cols].bitcast(FP8X4),
                     scales=scales[:, cols],
-                    in_=w1_grouped[q][:, i * width * PACK : (i + 1) * width * PACK],
+                    in_=w1_grouped[q][:, a * PACK : b * PACK],
                 )
             w1_codes[q] = codes
             w1_scales[q] = scales
 
-        w2_grouped = keep.tile([P, E, N, PACK], BF16, name="w2_grouped", align_bytes=64)
-        w2_codes = keep.tile([P, E * N], U32, name="w2_codes", align_bytes=64)
-        w2_scales = keep.tile([P, E * N], U8, name="w2_scales", align_bytes=64)
-
-        def second_weights(first, last, copy):
-            for e in range(first, last):
-                copy(
-                    w2_grouped[:, e].rearrange("p (c i) j -> p c j i", i=LINE),
-                    w2_raw[:, e].rearrange("p j (c i) -> p c j i", i=LINE),
-                )
-            cols = slice(first * N, last * N)
-            nc.vector.quantize_mx(
-                out=w2_codes[:, cols].bitcast(FP8X4),
-                scales=w2_scales[:, cols],
-                in_=w2_grouped[:, first:last].rearrange("p e n j -> p (e n j)"),
-            )
-
         hidden_sums = {}
 
-        def first_layer(e):
+        def first_layer_pass(q):
+            e, g = q // PASSES, q % PASSES
             for b in range(2):
+                if g == 0:
+                    hidden_sums[(e, b)] = psum_h.tile([P, TILES, HALF], F32, name="hidden_sums")
                 cols = slice(e * C + b * HALF, e * C + (b + 1) * HALF)
-                sums = psum_h.tile([P, TILES, HALF], F32, name="hidden_sums")
                 for t in range(TILES):
                     channels = slice(t * P, (t + 1) * P)
-                    for g in range(PASSES):
-                        q = e * PASSES + g
-                        nc.tensor.matmul_mx(
-                            out=sums[:, t, :],
-                            lhsT=w1_codes[q][:, channels].bitcast(FP8X4),
-                            lhsT_scale=w1_scales[q][:, channels],
-                            rhs=slot_codes[:, g, cols].bitcast(FP8X4),
-                            rhs_scale=slot_scales[SCALE_ROWS * g : P, cols],
-                            start=(g == 0),
-                            stop=(g == PASSES - 1),
-                        )
-                hidden_sums[(e, b)] = sums
+                    nc.tensor.matmul_mx(
+                        out=hidden_sums[(e, b)][:, t, :],
+                        lhsT=w1_codes[q][:, channels].bitcast(FP8X4),
+                        lhsT_scale=w1_scales[q][:, channels],
+                        rhs=slot_codes[g][:, cols].bitcast(FP8X4),
+                        rhs_scale=slot_scales[SCALE_ROWS * g : P, cols],
+                        start=(g == 0 and t == 0),
+                        stop=(g == PASSES - 1 and t == TILES - 1),
+                    )
 
-        y_sums = {}
-
-        def second_layer(e, b):
-            if e < E - 1:
-                place = place_of(GELU_OVER[e][b]) + b * HALF * PACK * 2
-                h = raws.tile([P, HALF * PACK], BF16, name=f"h{e}_{b}", offset=place, align_bytes=64)
-            else:
-                h = hidden.tile([P, HALF * PACK], BF16, name="h_last", align_bytes=64)
+        def gelu(e, b, h):
             nc.scalar.activation(
-                h[:].rearrange("p (s t) -> p s t", t=TILES), hidden_sums[(e, b)][:].rearrange("p t s -> p s t"), GELU
+                h.rearrange("p (s t) -> p s t", t=TILES), hidden_sums[(e, b)][:].rearrange("p t s -> p s t"), GELU
             )
-            codes = hidden.tile([P, HALF], U32, name="h_codes", align_bytes=64)
-            scales = hidden.tile([P, HALF], U8, name="h_scales", align_bytes=64)
+
+        def quantise_hidden(name, h, slots, place):
+            codes = raws.tile([P, slots], U32, name=name + "_codes", offset=place, align_bytes=64)
+            scales = keep.tile([P, slots], U8, name=name + "_scales", align_bytes=64)
             nc.vector.quantize_mx(out=codes[:].bitcast(FP8X4), scales=scales[:], in_=h[:])
-            if b == 0 or e == E - 1:
-                sums = psum_y.tile([P, C], F32, name="y_sums")
-                y_sums[(e, b)] = sums
-            else:
-                y_sums[(e, b)] = y_sums[(e, 0)]
-            channels = slice(e * N, (e + 1) * N)
+            return codes, scales
+
+        def second_layer(sums, weights, column, hidden):
+            channels = slice(column * N, (column + 1) * N)
             nc.tensor.matmul_mx(
-                out=y_sums[(e, b)][:, b * HALF : (b + 1) * HALF],
-                lhsT=w2_codes[:, channels].bitcast(FP8X4),
-                lhsT_scale=w2_scales[:, channels],
-                rhs=codes[:].bitcast(FP8X4),
-                rhs_scale=scales[:],
+                out=sums,
+                lhsT=weights[0][:, channels].bitcast(FP8X4),
+                lhsT_scale=weights[1][:, channels],
+                rhs=hidden[0][:].bitcast(FP8X4),
+                rhs_scale=hidden[1][:],
                 start=True,
                 stop=True,
             )
 
-        y_slots = keep.tile([P, SLOTS], F32, name="y_slots")
-
+        w2_rows = w2.rearrange("e (p j) n -> p e j n", j=PACK)
+        w2_raw = []
+        hidden_values = {}
+        hidden = {}
         for q in range(PIECES):
             interleave(q)
-            if q + RAW_PLACES < PIECES:
-                load_w1(q + RAW_PLACES)
-            elif q + RAW_PLACES == PIECES:
-                nc.sync.dma_start(w2_raw[:, E - LATE_EXPERTS :], w2_rows[:, E - LATE_EXPERTS :])
+            if q == 0:
+                load_w1(PIECES - 1)
+                for first, last in ((0, 2), (2, 3), (3, 4)):
+                    place = W2_PLACE + first * W2_BYTES
+                    raw = raws.tile([P, last - first, PACK, N], F32, name=f"w2_raw{first}", offset=place, align_bytes=64)
+                    nc.sync.dma_start(raw[:], w2_rows[:, first:last])
+                    w2_raw.append(raw)
                 nc.sync.dma_start(pos1_list[:], pos1)
                 nc.sync.dma_start(pos2_list[:], pos2)
                 nc.sync.dma_start(gate_rows[:], gate.rearrange("r n t -> n r t"))
             quantise(q)
-            if q == PASSES - 1:
-                second_weights(0, E - LATE_EXPERTS, nc.scalar.copy)
-            if q == PIECES - 1:
-                second_weights(E - LATE_EXPERTS, E, nc.vector.tensor_copy)
-            if q % PASSES == PASSES - 1:
-                first_layer(q // PASSES)
+            if q == 1:
+                codes = raws.tile([P, SLOTS], U32, name="slot_codes2", offset=LAST_CODES_PLACE, align_bytes=64)
+                gather_codes(PASSES - 1, codes)
+            first_layer_pass(q)
             for e in range(E - 1):
-                for b in range(2):
-                    if q == GELU_OVER[e][b]:
-                        second_layer(e, b)
-                        if b == 1:
-                            nc.scalar.copy(y_slots[:, e * C : (e + 1) * C], y_sums[(e, 0)][:])
+                if q == GELU_OVER[e]:
+                    h = raws.tile([P, C * PACK], BF16, name=f"h{e}", offset=place_of(q), align_bytes=64)
+                    for b in range(2):
+                        gelu(e, b, h[:, b * HALF * PACK : (b + 1) * HALF * PACK])
+                    hidden_values[e] = h
+                if q == GELU_OVER[e] + 1:
+                    hidden[e] = quantise_hidden(f"h{e}", hidden_values[e], C, place_of(q))
+
+        w2_grouped = keep.tile([P, E, N, PACK], BF16, name="w2_grouped", align_bytes=64)
+        for e, raw, copy in (
+            (0, w2_raw[0][:, 0], nc.scalar.copy),
+            (1, w2_raw[0][:, 1], nc.scalar.copy),
+            (2, w2_raw[1][:, 0], nc.vector.tensor_copy),
+            (3, w2_raw[2][:, 0], nc.vector.tensor_copy),
+        ):
+            copy(
+                w2_grouped[:, e].rearrange("p (c i) j -> p c j i", i=LINE),
+                raw.rearrange("p j (c i) -> p c j i", i=LINE),
+            )
+        last_place = W2_PLACE + (E - 1) * W2_BYTES
+        w2_quantised = []
+        for pair in range(2):
+            if pair == 0:
+                codes = raws.tile([P, 2 * N], U32, name="w2_codes0", offset=last_place, align_bytes=64)
+            else:
+                codes = keep.tile([P, 2 * N], U32, name="w2_codes1", align_bytes=64)
+            scales = keep.tile([P, 2 * N], U8, name=f"w2_scales{pair}", align_bytes=64)
+            nc.vector.quantize_mx(
+                out=codes[:].bitcast(FP8X4),
+                scales=scales[:],
+                in_=w2_grouped[:, 2 * pair : 2 * pair + 2].rearrange("p e n j -> p (e n j)"),
+            )
+            w2_quantised.append((codes, scales))
+
+        last_hidden = []
         for b in range(2):
-            second_layer(E - 1, b)
-        for b, copy in ((0, nc.vector.tensor_copy), (1, nc.scalar.copy)):
-            cols = slice((E - 1) * C + b * HALF, (E - 1) * C + (b + 1) * HALF)
-            copy(y_slots[:, cols], y_sums[(E - 1, b)][:, b * HALF : (b + 1) * HALF])
+            h = raws.tile([P, HALF * PACK], BF16, name=f"h_last{b}", offset=W2_PLACE + b * HALF * PACK * 2, align_bytes=64)
+            gelu(E - 1, b, h[:])
+            last_hidden.append(quantise_hidden(f"h_last{b}", h, HALF, last_place + 2 * N * 4 + b * HALF * 4))
+
+        y_slots = keep.tile([P, SLOTS], F32, name="y_slots")
+        y_first = psum_y.tile([P, 2 * C], F32, name="y_first")
+        for e in range(2):
+            second_layer(y_first[:, e * C : (e + 1) * C], w2_quantised[0], e, hidden[e])
+        y_third = psum_y.tile([P, C], F32, name="y_third")
+        second_layer(y_third[:], w2_quantised[1], 0, hidden[2])
+        y_last = []
+        for b in range(2):
+            sums = psum_y.tile([P, HALF], F32, name=f"y_last{b}")
+            second_layer(sums[:], w2_quantised[1], 1, last_hidden[b])
+            y_last.append(sums)
+        nc.scalar.copy(y_slots[:, : 2 * C], y_first[:])
+        nc.vector.tensor_copy(y_slots[:, 2 * C : 3 * C], y_third[:])
+        nc.scalar.copy(y_slots[:, 3 * C : 3 * C + HALF], y_last[0][:])
+        nc.vector.tensor_copy(y_slots[:, 3 * C + HALF :], y_last[1][:])
 
         first = keep.tile([P, T], F32, name="first")
         nc.vector.tensor_tensor(first[:], y_slots[:].indirect(pos1_list[:]), gate_rows[:, 0, :], MULT)
-        width = T // 2
-        token_halves = [slice(i * width, (i + 1) * width) for i in range(2)]
+        token_halves = [slice(0, 384), slice(384, T)]
         second = keep.tile([P, T], F32, name="second")
         for tokens in token_halves:
             entries = pos2_list[:, tokens.start // LIST_ROWS : tokens.stop // LIST_ROWS]
             nc.vector.tensor_tensor(second[:, tokens], y_slots[:].indirect(entries), gate_rows[:, 1, tokens], MULT)
+        total = keep.tile([P, T], F32, name="total")
         for tokens in token_halves:
-            total = hidden.tile([P, width], F32, name="total")
-            nc.vector.tensor_tensor(total[:], first[:, tokens], second[:, tokens], ADD)
-            nc.sync.dma_start(out[:, tokens], total[:])
+            nc.vector.tensor_tensor(total[:, tokens], first[:, tokens], second[:, tokens], ADD)
+            nc.sync.dma_start(out[:, tokens], total[:, tokens])

@@ -32,14 +32,19 @@ SCALE_ROWS = 4
 WINDOW = 1408
 
 VECTOR_TOKENS = [320, 64, 64]
-VECTOR_GROUPS = [0, 0, 0, 0, 96, 64, 56, 88, 76, 76, 76]
+VECTOR_GROUPS = [0, 0, 0, 0, 32, 96, 64, 88, 76, 76, 76]
+GPSIMD_PIECES = [0, 1, 3]
+GPSIMD_GROUPS = 48
 
 RAW_BYTES = PACK * H * 4
 RAW_PLACES = 11
 W2_PLACE = RAW_PLACES * RAW_BYTES
 W2_BYTES = PACK * N * 4
 LAST_CODES_PLACE = W2_PLACE + E * W2_BYTES
-GELU_OVER = [3, 6, 9]
+GELU_OVER = [4, 6, 9]
+GROUP_BYTES = PACK * H * 2
+X_GROUP_PLACE = {1: LAST_CODES_PLACE + 2 * GROUP_BYTES, 2: LAST_CODES_PLACE + GROUP_BYTES // 2}
+W1_GROUP_PLACE = {0: X_GROUP_PLACE[1], 1: X_GROUP_PLACE[2], 3: LAST_CODES_PLACE + GROUP_BYTES}
 LAST_CUTS = [0, 256, 384, 512]
 
 
@@ -58,7 +63,7 @@ def tile_routed_moe_kernel(tc, xT, w1, w2, gate, offs, pos1, pos2, out):
     nc = tc.nc
     with ExitStack() as ctx:
         keep = ctx.enter_context(tc.tile_pool(name="keep", bufs=1))
-        token_groups = ctx.enter_context(tc.tile_pool(name="token_groups", bufs=PASSES))
+        token_groups = ctx.enter_context(tc.tile_pool(name="token_groups", bufs=1))
         raws = ctx.enter_context(tc.tile_pool(name="raws", bufs=1))
         w1_groups = ctx.enter_context(tc.tile_pool(name="w1_groups", bufs=5))
         psum_h = ctx.enter_context(tc.psum_pool(name="psum_h", bufs=4))
@@ -109,7 +114,10 @@ def tile_routed_moe_kernel(tc, xT, w1, w2, gate, offs, pos1, pos2, out):
 
         slot_scales = keep.tile([P, SLOTS], U8, name="slot_scales", align_bytes=64)
         for g in range(PASSES):
-            grouped = token_groups.tile([P, T, PACK], BF16, name="grouped", align_bytes=64)
+            if g in X_GROUP_PLACE:
+                grouped = raws.tile([P, T, PACK], BF16, name=f"grouped{g}", offset=X_GROUP_PLACE[g], align_bytes=64)
+            else:
+                grouped = token_groups.tile([P, T, PACK], BF16, name="grouped", align_bytes=64)
             shared_copy(
                 nc,
                 grouped[:].rearrange("p (c i) j -> p c j i", i=LINE),
@@ -131,13 +139,25 @@ def tile_routed_moe_kernel(tc, xT, w1, w2, gate, offs, pos1, pos2, out):
         w1_scales = {}
 
         def interleave(q):
-            if q == 1:
-                grouped = raws.tile([P, H * PACK], BF16, name="w1_grouped1", offset=LAST_CODES_PLACE, align_bytes=64)
+            if q in W1_GROUP_PLACE:
+                grouped = raws.tile([P, H * PACK], BF16, name=f"w1_grouped{q}", offset=W1_GROUP_PLACE[q], align_bytes=64)
             else:
                 grouped = w1_groups.tile([P, H * PACK], BF16, name="w1_grouped", align_bytes=64)
             dst = grouped[:].rearrange("p (t m j) -> p m j t", t=TILES, j=PACK)
             src = w1_raw[q][:].rearrange("p j (m t) -> p m j t", t=TILES)
-            if q < PIECES - 1:
+            if q in GPSIMD_PIECES:
+                for a in range(0, GPSIMD_GROUPS, GPSIMD_GROUPS // 2):
+                    part = slice(a, a + GPSIMD_GROUPS // 2)
+                    nc.gpsimd.tensor_scalar(
+                        dst[:, part].rearrange("p m j t -> p t m j"),
+                        src[:, part].rearrange("p m j t -> p t m j"),
+                        1.0,
+                        0.0,
+                        MULT,
+                        ADD,
+                    )
+                nc.scalar.copy(dst[:, GPSIMD_GROUPS:], src[:, GPSIMD_GROUPS:])
+            elif q < PIECES - 1:
                 shared_copy(nc, dst, src, VECTOR_GROUPS[q])
             else:
                 nc.vector.tensor_copy(dst[:, :, :, :2], src[:, :, :, :2])

@@ -45,7 +45,8 @@ GELU_OVER = [4, 6, 9]
 GROUP_BYTES = PACK * H * 2
 X_GROUP_PLACE = {1: LAST_CODES_PLACE + 2 * GROUP_BYTES, 2: LAST_CODES_PLACE + GROUP_BYTES // 2}
 W1_GROUP_PLACE = {0: X_GROUP_PLACE[1], 1: X_GROUP_PLACE[2], 3: LAST_CODES_PLACE + GROUP_BYTES}
-LAST_CUTS = [0, 256, 384, 512]
+LAST_VECTOR_GROUPS = 40
+LAST_CUTS = [0, 256, 512]
 
 
 def place_of(q):
@@ -161,7 +162,7 @@ def tile_routed_moe_kernel(tc, xT, w1, w2, gate, offs, pos1, pos2, out):
                 shared_copy(nc, dst, src, VECTOR_GROUPS[q])
             else:
                 nc.vector.tensor_copy(dst[:, :, :, :2], src[:, :, :, :2])
-                nc.scalar.copy(dst[:, :, :, 2:], src[:, :, :, 2:])
+                shared_copy(nc, dst[:, :, :, 2:], src[:, :, :, 2:], LAST_VECTOR_GROUPS)
             w1_grouped[q] = grouped
 
         def quantise(q):
@@ -254,7 +255,7 @@ def tile_routed_moe_kernel(tc, xT, w1, w2, gate, offs, pos1, pos2, out):
         w2_grouped = keep.tile([P, E, N, PACK], BF16, name="w2_grouped", align_bytes=64)
         for e, raw, copy in (
             (0, w2_raw[0][:, 0], nc.scalar.copy),
-            (1, w2_raw[0][:, 1], nc.scalar.copy),
+            (1, w2_raw[0][:, 1], nc.vector.tensor_copy),
             (2, w2_raw[1][:, 0], nc.vector.tensor_copy),
             (3, w2_raw[2][:, 0], nc.vector.tensor_copy),
         ):

@@ -32,7 +32,7 @@ SCALE_ROWS = 4
 WINDOW = 1408
 
 VECTOR_TOKENS = [320, 64, 64]
-VECTOR_GROUPS = [0, 0, 0, 0, 32, 96, 64, 88, 76, 76, 76]
+VECTOR_GROUPS = [0, 0, 0, 0, 32, 96, 64, 88, 76, 88, 88]
 GPSIMD_PIECES = [0, 1, 3]
 GPSIMD_GROUPS = 48
 
@@ -168,7 +168,7 @@ def tile_routed_moe_kernel(tc, xT, w1, w2, gate, offs, pos1, pos2, out):
         def quantise(q):
             codes = keep.tile([P, H], U32, name=f"w1_codes{q}", align_bytes=64)
             scales = keep.tile([P, H], U8, name=f"w1_scales{q}", align_bytes=64)
-            cuts = LAST_CUTS if q == PIECES - 1 else [0, H]
+            cuts = LAST_CUTS if q in (PIECES - 1, PIECES - 1 - PASSES) else [0, H]
             for a, b in zip(cuts[:-1], cuts[1:]):
                 cols = slice(a, b)
                 nc.vector.quantize_mx(

@@ -32,7 +32,7 @@ SCALE_ROWS = 4
 WINDOW = 1408
 
 VECTOR_TOKENS = [320, 64, 64]
-VECTOR_GROUPS = [0, 0, 0, 0, 32, 96, 64, 88, 76, 88, 88]
+VECTOR_GROUPS = [0, 0, 0, 0, 32, 96, 64, 88, 88, 88, 88]
 GPSIMD_PIECES = [0, 1, 3]
 GPSIMD_GROUPS = 48
 
@@ -45,7 +45,7 @@ GELU_OVER = [4, 6, 9]
 GROUP_BYTES = PACK * H * 2
 X_GROUP_PLACE = {1: LAST_CODES_PLACE + 2 * GROUP_BYTES, 2: LAST_CODES_PLACE + GROUP_BYTES // 2}
 W1_GROUP_PLACE = {0: X_GROUP_PLACE[1], 1: X_GROUP_PLACE[2], 3: LAST_CODES_PLACE + GROUP_BYTES}
-LAST_VECTOR_GROUPS = 40
+LAST_VECTOR_GROUPS = 48
 LAST_CUTS = [0, 256, 512]
 
 

@@ -30,43 +30,25 @@ LIST_ROWS = 16
 
 SCALE_ROWS = 4
 WINDOW = 1408
+COPY = mybir.ActivationFunctionType.Copy
 
-VECTOR_TOKENS = [320, 64, 64]
-VECTOR_GROUPS = [0, 0, 0, 0, 32, 96, 64, 88, 88, 88, 88]
-GPSIMD_PIECES = [0, 1, 3]
-GPSIMD_GROUPS = 48
-
-RAW_BYTES = PACK * H * 4
-RAW_PLACES = 11
-W2_PLACE = RAW_PLACES * RAW_BYTES
+PAIR = 2
+PIECE_BYTES = PACK * H * 4
+PAIR_BYTES = PAIR * P * PACK * 2
+LOADS = [[0, 1], [2, 3], [4, 5], [6], [7], [8], [9], [10]]
+LAST = PIECES - 1
 W2_BYTES = PACK * N * 4
-LAST_CODES_PLACE = W2_PLACE + E * W2_BYTES
-GELU_OVER = [4, 6, 9]
-GROUP_BYTES = PACK * H * 2
-X_GROUP_PLACE = {1: LAST_CODES_PLACE + 2 * GROUP_BYTES, 2: LAST_CODES_PLACE + GROUP_BYTES // 2}
-W1_GROUP_PLACE = {0: X_GROUP_PLACE[1], 1: X_GROUP_PLACE[2], 3: LAST_CODES_PLACE + GROUP_BYTES}
-LAST_VECTOR_GROUPS = 48
-LAST_CUTS = [0, 256, 512]
-
-
-def place_of(q):
-    return (PASSES + q) % RAW_PLACES * RAW_BYTES
-
-
-def shared_copy(nc, dst, src, cut):
-    if cut > 0:
-        nc.vector.tensor_copy(dst[:, :cut], src[:, :cut])
-    if cut < dst.shape[1]:
-        nc.scalar.copy(dst[:, cut:], src[:, cut:])
+GELU_OVER = [5, 7, 9]
+EXTRA_COLUMNS = {3: 64, 4: 32, 5: 32, 6: 32, 7: 32, 8: 32, 9: 32, 10: 32}
+VECTOR_TOKENS = [320, 64, 0]
+GPSIMD_COLUMNS = 96
 
 
 def tile_routed_moe_kernel(tc, xT, w1, w2, gate, offs, pos1, pos2, out):
     nc = tc.nc
     with ExitStack() as ctx:
         keep = ctx.enter_context(tc.tile_pool(name="keep", bufs=1))
-        token_groups = ctx.enter_context(tc.tile_pool(name="token_groups", bufs=1))
-        raws = ctx.enter_context(tc.tile_pool(name="raws", bufs=1))
-        w1_groups = ctx.enter_context(tc.tile_pool(name="w1_groups", bufs=5))
+        arena = ctx.enter_context(tc.tile_pool(name="arena", bufs=1))
         psum_h = ctx.enter_context(tc.psum_pool(name="psum_h", bufs=4))
         psum_y = ctx.enter_context(tc.psum_pool(name="psum_y", bufs=1))
 
@@ -75,119 +57,124 @@ def tile_routed_moe_kernel(tc, xT, w1, w2, gate, offs, pos1, pos2, out):
         pos2_list = keep.tile([P, T // LIST_ROWS], U16, name="pos2_list")
         gate_rows = keep.tile([P, 2, T], F32, name="gate_rows")
 
-        token_codes = keep.tile([P, PASSES, WINDOW], U32, name="token_codes", align_bytes=64)
-        nc.vector.memset(token_codes[:, :, T:].bitcast(I32), 0)
-        token_scales = keep.tile([P, WINDOW], U8, name="token_scales", align_bytes=64)
-        nc.gpsimd.memset(token_scales[:], 0)
-
         warm = keep.tile([P, 2], F32, name="warm")
         nc.vector.memset(warm[:, :1], 0.0)
         nc.scalar.activation(warm[:, 1:], warm[:, :1], GELU)
 
-        x_raw = []
-        w1_raw = {}
+        token_codes = keep.tile([P, PASSES, WINDOW], U32, name="token_codes", align_bytes=64)
+        nc.vector.memset(token_codes[:, :, T:].bitcast(I32), 0)
+        token_scales = keep.tile([P, WINDOW], U8, name="token_scales", align_bytes=64)
+        nc.vector.memset(token_scales[:].bitcast(I32), 0)
 
-        def load_x(g):
-            raw = raws.tile([P, PACK, T], F32, name=f"x_raw{g}", offset=g * RAW_BYTES, align_bytes=64)
+        def placed(name, shape, dtype, offset):
+            return arena.tile(shape, dtype, name=name, offset=offset, align_bytes=64)
+
+        x_grouped_place = [PASSES * PIECE_BYTES, PASSES * PIECE_BYTES, PIECE_BYTES]
+        load_place = []
+        place = PASSES * PIECE_BYTES + 2 * PAIR_BYTES
+        for pieces in LOADS:
+            load_place.append(place)
+            place += len(pieces) * PIECE_BYTES + PAIR_BYTES
+        last_place = [place, place + PIECE_BYTES // 2]
+        w2_place = [place + PIECE_BYTES + e * W2_BYTES for e in range(E)]
+        load_of = {q: i for i, pieces in enumerate(LOADS) for q in pieces}
+        load_of[LAST] = len(LOADS)
+
+        x_raw = []
+        for g in range(PASSES):
+            raw = placed(f"x_raw{g}", [P, PACK, T], F32, g * PIECE_BYTES)
             nc.sync.dma_start(raw[:], xT[g * K_PASS : (g + 1) * K_PASS, :].rearrange("(p j) t -> p j t", j=PACK))
             x_raw.append(raw)
+            if g == 0:
+                nc.sync.dma_start(offs_list[:], offs)
+        w1_rows = w1.rearrange("e (g p j) c -> p (e g) j c", p=P, j=PACK)
+        w1_raw = {}
+        for i, pieces in enumerate(LOADS):
+            raw = placed(f"w1_raw{i}", [P, len(pieces), PACK, H], F32, load_place[i])
+            nc.sync.dma_start(raw[:], w1_rows[:, pieces[0] : pieces[-1] + 1])
+            for n, q in enumerate(pieces):
+                w1_raw[q] = raw[:, n]
+        last_raw = []
+        for half in range(2):
+            raw = placed(f"last_raw{half}", [P, PACK, H // 2], F32, last_place[half])
+            nc.sync.dma_start(raw[:], w1_rows[:, LAST, :, half * (H // 2) : (half + 1) * (H // 2)])
+            last_raw.append(raw)
+        w2_rows = w2.rearrange("e (p j) n -> p e j n", j=PACK)
+        w2_raw = []
+        for e in range(E):
+            raw = placed(f"w2_raw{e}", [P, PACK, N], F32, w2_place[e])
+            nc.sync.dma_start(raw[:], w2_rows[:, e])
+            w2_raw.append(raw)
+        nc.sync.dma_start(pos1_list[:], pos1)
+        nc.sync.dma_start(pos2_list[:], pos2)
+        nc.sync.dma_start(gate_rows[:], gate.rearrange("r n t -> n r t"))
 
-        def load_w1(q):
-            e, g = q // PASSES, q % PASSES
-            raw = raws.tile([P, PACK, H], F32, name=f"w1_raw{q}", offset=place_of(q), align_bytes=64)
-            src = w1[e, g * K_PASS : (g + 1) * K_PASS, :].rearrange("(p j) c -> p j c", j=PACK)
-            nc.sync.dma_start(raw[:], src)
-            w1_raw[q] = raw
+        def by_lines(dst, src):
+            return dst.rearrange("p (c i) j -> p c j i", i=LINE), src.rearrange("p j (c i) -> p c j i", i=LINE)
 
-        load_x(0)
-        nc.sync.dma_start(offs_list[:], offs)
-        load_x(1)
-        load_w1(0)
-        load_x(2)
-        for q in range(1, RAW_PLACES - PASSES):
-            load_w1(q)
-
-        slot_codes = {}
-
-        def gather_codes(g, codes):
-            nc.vector.tensor_copy(codes[:], token_codes[:, g, :].indirect(offs_list[:]))
-            slot_codes[g] = codes
-
+        slot_codes = []
         slot_scales = keep.tile([P, SLOTS], U8, name="slot_scales", align_bytes=64)
         for g in range(PASSES):
-            if g in X_GROUP_PLACE:
-                grouped = raws.tile([P, T, PACK], BF16, name=f"grouped{g}", offset=X_GROUP_PLACE[g], align_bytes=64)
-            else:
-                grouped = token_groups.tile([P, T, PACK], BF16, name="grouped", align_bytes=64)
-            shared_copy(
-                nc,
-                grouped[:].rearrange("p (c i) j -> p c j i", i=LINE),
-                x_raw[g][:].rearrange("p j (c i) -> p c j i", i=LINE),
-                VECTOR_TOKENS[g] // LINE,
-            )
+            grouped = placed(f"x_grouped{g}", [P, T, PACK], BF16, x_grouped_place[g])
+            cut = VECTOR_TOKENS[g]
+            if cut:
+                nc.vector.tensor_copy(*by_lines(grouped[:, :cut], x_raw[g][:, :, :cut]))
+            nc.scalar.copy(*by_lines(grouped[:, cut:], x_raw[g][:, :, cut:]))
             nc.vector.quantize_mx(
                 out=token_codes[:, g, :T].bitcast(FP8X4),
                 scales=token_scales[SCALE_ROWS * g : P, :T],
                 in_=grouped[:].rearrange("p t j -> p (t j)"),
             )
-            if g < PASSES - 1:
-                gather_codes(g, keep.tile([P, SLOTS], U32, name=f"slot_codes{g}", align_bytes=64))
-            load_w1(RAW_PLACES - PASSES + g)
-        nc.vector.tensor_copy(slot_scales[:], token_scales[:].indirect(offs_list[:]))
+            if g == PASSES - 1:
+                nc.vector.tensor_copy(slot_scales[:], token_scales[:].indirect(offs_list[:]))
+            codes = keep.tile([P, SLOTS], U32, name=f"slot_codes{g}", align_bytes=64)
+            nc.vector.tensor_copy(codes[:], token_codes[:, g, :].indirect(offs_list[:]))
+            slot_codes.append(codes)
 
-        w1_grouped = {}
+        def pair_views(grouped, raw, pair, first):
+            src = raw.rearrange("p j (m t) -> p m j t", t=TILES)[:, :, :, PAIR * pair : PAIR * (pair + 1)]
+            dst = grouped[:].rearrange("p t m j -> p m j t")[:, first : first + src.shape[1]]
+            return dst, src
+
+        def pair_place(q, pair):
+            i = load_of[q]
+            if i == 0:
+                return x_grouped_place[-1] + q * PAIR_BYTES if pair else (PASSES - 1) * PIECE_BYTES + q * PAIR_BYTES
+            n = q - LOADS[i - 1][-1] - 1
+            if pair == 0 and q == LAST - 1:
+                return load_place[i] - PAIR_BYTES - PAIR_BYTES // 2
+            if pair == 1 and n == 0 and i > 1:
+                return pair_place(q - 1, 1)
+            return load_place[i - 1] + (2 * n + 2 - pair) * PAIR_BYTES
+
         w1_codes = {}
         w1_scales = {}
 
-        def interleave(q):
-            if q in W1_GROUP_PLACE:
-                grouped = raws.tile([P, H * PACK], BF16, name=f"w1_grouped{q}", offset=W1_GROUP_PLACE[q], align_bytes=64)
+        def new_codes(q):
+            if q == LAST - PASSES:
+                w1_codes[q] = placed(f"w1_codes{q}", [P, H], U32, load_place[load_of[LAST - 1]] - PAIR_BYTES)
             else:
-                grouped = w1_groups.tile([P, H * PACK], BF16, name="w1_grouped", align_bytes=64)
-            dst = grouped[:].rearrange("p (t m j) -> p m j t", t=TILES, j=PACK)
-            src = w1_raw[q][:].rearrange("p j (m t) -> p m j t", t=TILES)
-            if q in GPSIMD_PIECES:
-                for a in range(0, GPSIMD_GROUPS, GPSIMD_GROUPS // 2):
-                    part = slice(a, a + GPSIMD_GROUPS // 2)
-                    nc.gpsimd.tensor_scalar(
-                        dst[:, part].rearrange("p m j t -> p t m j"),
-                        src[:, part].rearrange("p m j t -> p t m j"),
-                        1.0,
-                        0.0,
-                        MULT,
-                        ADD,
-                    )
-                nc.scalar.copy(dst[:, GPSIMD_GROUPS:], src[:, GPSIMD_GROUPS:])
-            elif q < PIECES - 1:
-                shared_copy(nc, dst, src, VECTOR_GROUPS[q])
-            else:
-                nc.vector.tensor_copy(dst[:, :, :, :2], src[:, :, :, :2])
-                shared_copy(nc, dst[:, :, :, 2:], src[:, :, :, 2:], LAST_VECTOR_GROUPS)
-            w1_grouped[q] = grouped
+                w1_codes[q] = keep.tile([P, H], U32, name=f"w1_codes{q}", align_bytes=64)
+            w1_scales[q] = keep.tile([P, H], U8, name=f"w1_scales{q}", align_bytes=64)
 
-        def quantise(q):
-            codes = keep.tile([P, H], U32, name=f"w1_codes{q}", align_bytes=64)
-            scales = keep.tile([P, H], U8, name=f"w1_scales{q}", align_bytes=64)
-            cuts = LAST_CUTS if q in (PIECES - 1, PIECES - 1 - PASSES) else [0, H]
-            for a, b in zip(cuts[:-1], cuts[1:]):
-                cols = slice(a, b)
-                nc.vector.quantize_mx(
-                    out=codes[:, cols].bitcast(FP8X4),
-                    scales=scales[:, cols],
-                    in_=w1_grouped[q][:, a * PACK : b * PACK],
-                )
-            w1_codes[q] = codes
-            w1_scales[q] = scales
+        def quantise(q, grouped, first_tile, tiles):
+            cols = slice(first_tile * P, (first_tile + tiles) * P)
+            part = grouped[:, first_tile % PAIR : first_tile % PAIR + tiles]
+            nc.vector.quantize_mx(
+                out=w1_codes[q][:, cols].bitcast(FP8X4),
+                scales=w1_scales[q][:, cols],
+                in_=part.rearrange("p t m j -> p (t m j)"),
+            )
 
         hidden_sums = {}
 
-        def first_layer_pass(q):
+        def first_layer_pass(q, orders):
             e, g = q // PASSES, q % PASSES
             for b in range(2):
                 if g == 0:
                     hidden_sums[(e, b)] = psum_h.tile([P, TILES, HALF], F32, name="hidden_sums")
                 cols = slice(e * C + b * HALF, e * C + (b + 1) * HALF)
-                for t in range(TILES):
+                for n, t in enumerate(orders[b]):
                     channels = slice(t * P, (t + 1) * P)
                     nc.tensor.matmul_mx(
                         out=hidden_sums[(e, b)][:, t, :],
@@ -195,8 +182,8 @@ def tile_routed_moe_kernel(tc, xT, w1, w2, gate, offs, pos1, pos2, out):
                         lhsT_scale=w1_scales[q][:, channels],
                         rhs=slot_codes[g][:, cols].bitcast(FP8X4),
                         rhs_scale=slot_scales[SCALE_ROWS * g : P, cols],
-                        start=(g == 0 and t == 0),
-                        stop=(g == PASSES - 1 and t == TILES - 1),
+                        start=(g == 0 and n == 0),
+                        stop=(g == PASSES - 1 and n == TILES - 1),
                     )
 
         def gelu(e, b, h):
@@ -204,110 +191,136 @@ def tile_routed_moe_kernel(tc, xT, w1, w2, gate, offs, pos1, pos2, out):
                 h.rearrange("p (s t) -> p s t", t=TILES), hidden_sums[(e, b)][:].rearrange("p t s -> p s t"), GELU
             )
 
-        def quantise_hidden(name, h, slots, place):
-            codes = raws.tile([P, slots], U32, name=name + "_codes", offset=place, align_bytes=64)
-            scales = keep.tile([P, slots], U8, name=name + "_scales", align_bytes=64)
-            nc.vector.quantize_mx(out=codes[:].bitcast(FP8X4), scales=scales[:], in_=h[:])
+        def quantise_whole(name, values, columns, place=None):
+            if place is None:
+                codes = keep.tile([P, columns], U32, name=name + "_codes", align_bytes=64)
+            else:
+                codes = placed(name + "_codes", [P, columns], U32, place)
+            scales = keep.tile([P, columns], U8, name=name + "_scales", align_bytes=64)
+            nc.vector.quantize_mx(out=codes[:].bitcast(FP8X4), scales=scales[:], in_=values)
             return codes, scales
 
-        def second_layer(sums, weights, column, hidden):
-            channels = slice(column * N, (column + 1) * N)
+        def second_layer(sums, e, hidden):
+            codes, scales = w2_quantised[e // 2]
+            channels = slice(e % 2 * N, (e % 2 + 1) * N)
             nc.tensor.matmul_mx(
                 out=sums,
-                lhsT=weights[0][:, channels].bitcast(FP8X4),
-                lhsT_scale=weights[1][:, channels],
+                lhsT=codes[:, channels].bitcast(FP8X4),
+                lhsT_scale=scales[:, channels],
                 rhs=hidden[0][:].bitcast(FP8X4),
                 rhs_scale=hidden[1][:],
                 start=True,
                 stop=True,
             )
 
-        w2_rows = w2.rearrange("e (p j) n -> p e j n", j=PACK)
-        w2_raw = []
-        hidden_values = {}
         hidden = {}
-        for q in range(PIECES):
-            interleave(q)
-            if q == 0:
-                load_w1(PIECES - 1)
-                for first, last in ((0, 2), (2, 3), (3, 4)):
-                    place = W2_PLACE + first * W2_BYTES
-                    raw = raws.tile([P, last - first, PACK, N], F32, name=f"w2_raw{first}", offset=place, align_bytes=64)
-                    nc.sync.dma_start(raw[:], w2_rows[:, first:last])
-                    w2_raw.append(raw)
-                nc.sync.dma_start(pos1_list[:], pos1)
-                nc.sync.dma_start(pos2_list[:], pos2)
-                nc.sync.dma_start(gate_rows[:], gate.rearrange("r n t -> n r t"))
-            quantise(q)
-            if q == 1:
-                codes = raws.tile([P, SLOTS], U32, name="slot_codes2", offset=LAST_CODES_PLACE, align_bytes=64)
-                gather_codes(PASSES - 1, codes)
-            first_layer_pass(q)
+        hidden_values = {}
+        w1_pairs = {}
+
+        def interleave(q):
+            pairs = [placed(f"w1_pair{q}_{pair}", [P, PAIR, P, PACK], BF16, pair_place(q, pair)) for pair in range(2)]
+            low = pair_views(pairs[0], w1_raw[q], 0, 0)
+            high = pair_views(pairs[1], w1_raw[q], 1, 0)
+            if load_of[q] == 0:
+                cut = GPSIMD_COLUMNS
+                order = "p m j t -> p t m j"
+                nc.gpsimd.tensor_scalar(
+                    high[0][:, :cut].rearrange(order), high[1][:, :cut].rearrange(order), 1.0, 0.0, MULT, ADD
+                )
+                nc.scalar.copy(*low)
+                nc.scalar.copy(high[0][:, cut:], high[1][:, cut:])
+            elif q == 2:
+                nc.scalar.copy(*low)
+                nc.scalar.copy(*high)
+            else:
+                nc.vector.tensor_copy(*high)
+                cut = EXTRA_COLUMNS.get(q, 0)
+                if cut:
+                    nc.vector.tensor_copy(low[0][:, :cut], low[1][:, :cut])
+                nc.scalar.copy(low[0][:, cut:], low[1][:, cut:])
+            w1_pairs[q] = pairs
+
+        for q in range(LAST):
+            if q == LOADS[load_of[q]][0]:
+                for piece in LOADS[load_of[q]]:
+                    interleave(piece)
+            pairs = w1_pairs[q]
+            new_codes(q)
+            quantise(q, pairs[1], PAIR, PAIR)
+            quantise(q, pairs[0], 0, PAIR)
+            first_layer_pass(q, [[2, 3, 0, 1]] * 2)
             for e in range(E - 1):
                 if q == GELU_OVER[e]:
-                    h = raws.tile([P, C * PACK], BF16, name=f"h{e}", offset=place_of(q), align_bytes=64)
+                    h = placed(f"h{e}", [P, C * PACK], BF16, load_place[load_of[q]])
                     for b in range(2):
                         gelu(e, b, h[:, b * HALF * PACK : (b + 1) * HALF * PACK])
                     hidden_values[e] = h
                 if q == GELU_OVER[e] + 1:
-                    hidden[e] = quantise_hidden(f"h{e}", hidden_values[e], C, place_of(q))
+                    hidden[e] = quantise_whole(f"h{e}", hidden_values[e][:], C, load_place[load_of[q]])
 
-        w2_grouped = keep.tile([P, E, N, PACK], BF16, name="w2_grouped", align_bytes=64)
-        for e, raw, copy in (
-            (0, w2_raw[0][:, 0], nc.scalar.copy),
-            (1, w2_raw[0][:, 1], nc.vector.tensor_copy),
-            (2, w2_raw[1][:, 0], nc.vector.tensor_copy),
-            (3, w2_raw[2][:, 0], nc.vector.tensor_copy),
-        ):
-            copy(
-                w2_grouped[:, e].rearrange("p (c i) j -> p c j i", i=LINE),
-                raw.rearrange("p j (c i) -> p c j i", i=LINE),
-            )
-        last_place = W2_PLACE + (E - 1) * W2_BYTES
-        w2_quantised = []
-        for pair in range(2):
-            if pair == 0:
-                codes = raws.tile([P, 2 * N], U32, name="w2_codes0", offset=last_place, align_bytes=64)
-            else:
-                codes = keep.tile([P, 2 * N], U32, name="w2_codes1", align_bytes=64)
-            scales = keep.tile([P, 2 * N], U8, name=f"w2_scales{pair}", align_bytes=64)
-            nc.vector.quantize_mx(
-                out=codes[:].bitcast(FP8X4),
-                scales=scales[:],
-                in_=w2_grouped[:, 2 * pair : 2 * pair + 2].rearrange("p e n j -> p (e n j)"),
-            )
-            w2_quantised.append((codes, scales))
+        pairs = [placed(f"last_pair{pair}", [P, PAIR, P, PACK], BF16, pair_place(LAST, pair)) for pair in range(2)]
+        for half in range(2):
+            nc.vector.tensor_copy(*pair_views(pairs[1], last_raw[half][:], 1, half * P // 2))
+            nc.scalar.copy(*pair_views(pairs[0], last_raw[half][:], 0, half * P // 2))
+        new_codes(LAST)
+        tile_order = [2, 3, 0, 1]
+        for t in tile_order:
+            quantise(LAST, pairs[t // PAIR], t, 1)
+        first_layer_pass(LAST, [tile_order, tile_order[::-1]])
 
+        w2_grouped = []
+        for pair, place in enumerate([last_place[1], pair_place(LAST, 0)]):
+            grouped = placed(f"w2_grouped{pair}", [P, 2, N, PACK], BF16, place)
+            w2_grouped.append(grouped)
+
+        def interleave_w2(e, copy):
+            copy(*by_lines(w2_grouped[e // 2][:, e % 2], w2_raw[e][:]))
+
+        def quantise_w2(pair):
+            return quantise_whole(f"w2_{pair}", w2_grouped[pair][:].rearrange("p e n j -> p (e n j)"), 2 * N)
+
+        interleave_w2(0, nc.scalar.copy)
+        last_h = []
+        for b in range(2):
+            h = placed(f"h_last{b}", [P, HALF * PACK], BF16, w2_place[0] + b * HALF * PACK * 2)
+            gelu(E - 1, b, h[:])
+            last_h.append(h)
+        interleave_w2(1, nc.vector.tensor_copy)
+        w2_quantised = [quantise_w2(0)]
+        interleave_w2(2, nc.vector.tensor_copy)
+        interleave_w2(3, nc.vector.tensor_copy)
+        w2_quantised.append(quantise_w2(1))
         last_hidden = []
         for b in range(2):
-            h = raws.tile([P, HALF * PACK], BF16, name=f"h_last{b}", offset=W2_PLACE + b * HALF * PACK * 2, align_bytes=64)
-            gelu(E - 1, b, h[:])
-            last_hidden.append(quantise_hidden(f"h_last{b}", h, HALF, last_place + 2 * N * 4 + b * HALF * 4))
+            last_hidden.append(quantise_whole(f"h_last{b}", last_h[b][:], HALF, w2_place[-1] + b * HALF * 4))
 
         y_slots = keep.tile([P, SLOTS], F32, name="y_slots")
         y_first = psum_y.tile([P, 2 * C], F32, name="y_first")
         for e in range(2):
-            second_layer(y_first[:, e * C : (e + 1) * C], w2_quantised[0], e, hidden[e])
+            second_layer(y_first[:, e * C : (e + 1) * C], e, hidden[e])
         y_third = psum_y.tile([P, C], F32, name="y_third")
-        second_layer(y_third[:], w2_quantised[1], 0, hidden[2])
+        second_layer(y_third[:], 2, hidden[2])
         y_last = []
         for b in range(2):
             sums = psum_y.tile([P, HALF], F32, name=f"y_last{b}")
-            second_layer(sums[:], w2_quantised[1], 1, last_hidden[b])
+            second_layer(sums[:], 3, last_hidden[b])
             y_last.append(sums)
         nc.scalar.copy(y_slots[:, : 2 * C], y_first[:])
-        nc.vector.tensor_copy(y_slots[:, 2 * C : 3 * C], y_third[:])
+        nc.scalar.copy(y_slots[:, 2 * C : 3 * C], y_third[:])
         nc.scalar.copy(y_slots[:, 3 * C : 3 * C + HALF], y_last[0][:])
         nc.vector.tensor_copy(y_slots[:, 3 * C + HALF :], y_last[1][:])
 
+        halves = [slice(0, T // 2), slice(T // 2, T)]
         first = keep.tile([P, T], F32, name="first")
         nc.vector.tensor_tensor(first[:], y_slots[:].indirect(pos1_list[:]), gate_rows[:, 0, :], MULT)
-        token_halves = [slice(0, 384), slice(384, T)]
-        second = keep.tile([P, T], F32, name="second")
-        for tokens in token_halves:
+        picked = keep.tile([P, T], F32, name="picked")
+        for tokens in halves:
             entries = pos2_list[:, tokens.start // LIST_ROWS : tokens.stop // LIST_ROWS]
-            nc.vector.tensor_tensor(second[:, tokens], y_slots[:].indirect(entries), gate_rows[:, 1, tokens], MULT)
+            nc.scalar.activation(picked[:, tokens], y_slots[:].indirect(entries), COPY)
+        second = keep.tile([P, T], F32, name="second")
+        for tokens in halves:
+            nc.vector.tensor_tensor(second[:, tokens], picked[:, tokens], gate_rows[:, 1, tokens], MULT)
         total = keep.tile([P, T], F32, name="total")
-        for tokens in token_halves:
+        for tokens in halves:
             nc.vector.tensor_tensor(total[:, tokens], first[:, tokens], second[:, tokens], ADD)
             nc.sync.dma_start(out[:, tokens], total[:, tokens])

@@ -35,13 +35,15 @@ COPY = mybir.ActivationFunctionType.Copy
 PAIR = 2
 PIECE_BYTES = PACK * H * 4
 PAIR_BYTES = PAIR * P * PACK * 2
-LOADS = [[0, 1], [2, 3], [4, 5], [6], [7], [8], [9], [10]]
+LOADS = [[0, 1], [2, 3], [4], [5], [6], [7], [8], [9], [10]]
 LAST = PIECES - 1
 W2_BYTES = PACK * N * 4
 GELU_OVER = [5, 7, 9]
-EXTRA_COLUMNS = {3: 64, 4: 32, 5: 32, 6: 32, 7: 32, 8: 32, 9: 32, 10: 32}
+VECTOR_COLUMNS = {2: 32, 3: 80, 4: 64, 5: 56, 6: 96, 7: 56, 8: 96, 9: 84}
+PAIRED = [10]
+EXTRA = 32
 VECTOR_TOKENS = [320, 64, 0]
-GPSIMD_COLUMNS = 96
+GPSIMD_COLUMNS = 48
 
 
 def tile_routed_moe_kernel(tc, xT, w1, w2, gate, offs, pos1, pos2, out):
@@ -58,13 +60,13 @@ def tile_routed_moe_kernel(tc, xT, w1, w2, gate, offs, pos1, pos2, out):
         gate_rows = keep.tile([P, 2, T], F32, name="gate_rows")
 
         warm = keep.tile([P, 2], F32, name="warm")
-        nc.vector.memset(warm[:, :1], 0.0)
+        nc.gpsimd.memset(warm[:, :1], 0.0)
         nc.scalar.activation(warm[:, 1:], warm[:, :1], GELU)
 
         token_codes = keep.tile([P, PASSES, WINDOW], U32, name="token_codes", align_bytes=64)
-        nc.vector.memset(token_codes[:, :, T:].bitcast(I32), 0)
+        nc.gpsimd.memset(token_codes[:, :, T:].bitcast(I32), 0)
         token_scales = keep.tile([P, WINDOW], U8, name="token_scales", align_bytes=64)
-        nc.vector.memset(token_scales[:].bitcast(I32), 0)
+        nc.gpsimd.memset(token_scales[:].bitcast(I32), 0)
 
         def placed(name, shape, dtype, offset):
             return arena.tile(shape, dtype, name=name, offset=offset, align_bytes=64)
@@ -119,7 +121,9 @@ def tile_routed_moe_kernel(tc, xT, w1, w2, gate, offs, pos1, pos2, out):
             cut = VECTOR_TOKENS[g]
             if cut:
                 nc.vector.tensor_copy(*by_lines(grouped[:, :cut], x_raw[g][:, :, :cut]))
-            nc.scalar.copy(*by_lines(grouped[:, cut:], x_raw[g][:, :, cut:]))
+            middle = (cut + T) // 2
+            for part in (slice(cut, middle), slice(middle, T)):
+                nc.scalar.copy(*by_lines(grouped[:, part], x_raw[g][:, :, part]))
             nc.vector.quantize_mx(
                 out=token_codes[:, g, :T].bitcast(FP8X4),
                 scales=token_scales[SCALE_ROWS * g : P, :T],
@@ -137,24 +141,13 @@ def tile_routed_moe_kernel(tc, xT, w1, w2, gate, offs, pos1, pos2, out):
             return dst, src
 
         def pair_place(q, pair):
-            i = load_of[q]
-            if i == 0:
-                return x_grouped_place[-1] + q * PAIR_BYTES if pair else (PASSES - 1) * PIECE_BYTES + q * PAIR_BYTES
-            n = q - LOADS[i - 1][-1] - 1
-            if pair == 0 and q == LAST - 1:
-                return load_place[i] - PAIR_BYTES - PAIR_BYTES // 2
-            if pair == 1 and n == 0 and i > 1:
-                return pair_place(q - 1, 1)
-            return load_place[i - 1] + (2 * n + 2 - pair) * PAIR_BYTES
+            return load_place[-1 - pair] + 2 * PAIR_BYTES
 
         w1_codes = {}
         w1_scales = {}
 
         def new_codes(q):
-            if q == LAST - PASSES:
-                w1_codes[q] = placed(f"w1_codes{q}", [P, H], U32, load_place[load_of[LAST - 1]] - PAIR_BYTES)
-            else:
-                w1_codes[q] = keep.tile([P, H], U32, name=f"w1_codes{q}", align_bytes=64)
+            w1_codes[q] = keep.tile([P, H], U32, name=f"w1_codes{q}", align_bytes=64)
             w1_scales[q] = keep.tile([P, H], U8, name=f"w1_scales{q}", align_bytes=64)
 
         def quantise(q, grouped, first_tile, tiles):
@@ -217,37 +210,46 @@ def tile_routed_moe_kernel(tc, xT, w1, w2, gate, offs, pos1, pos2, out):
         hidden_values = {}
         w1_pairs = {}
 
+        def piece_place(q):
+            i = load_of[q]
+            if i == 0:
+                return x_grouped_place[-1] + q * 2 * PAIR_BYTES
+            if i == 1:
+                return (q - LOADS[i][0]) * 2 * PAIR_BYTES
+            return load_place[i - 1] + (q - LOADS[i][0] + 1) * 2 * PAIR_BYTES
+
         def interleave(q):
-            pairs = [placed(f"w1_pair{q}_{pair}", [P, PAIR, P, PACK], BF16, pair_place(q, pair)) for pair in range(2)]
-            low = pair_views(pairs[0], w1_raw[q], 0, 0)
-            high = pair_views(pairs[1], w1_raw[q], 1, 0)
+            grouped = placed(f"w1_grouped{q}", [P, TILES, P, PACK], BF16, piece_place(q))
+            dst = grouped[:].rearrange("p t m j -> p m j t")
+            src = w1_raw[q].rearrange("p j (m t) -> p m j t", t=TILES)
+            cut = GPSIMD_COLUMNS if load_of[q] == 0 else VECTOR_COLUMNS.get(q, 0)
             if load_of[q] == 0:
-                cut = GPSIMD_COLUMNS
                 order = "p m j t -> p t m j"
                 nc.gpsimd.tensor_scalar(
-                    high[0][:, :cut].rearrange(order), high[1][:, :cut].rearrange(order), 1.0, 0.0, MULT, ADD
+                    dst[:, :cut].rearrange(order), src[:, :cut].rearrange(order), 1.0, 0.0, MULT, ADD
                 )
-                nc.scalar.copy(*low)
-                nc.scalar.copy(high[0][:, cut:], high[1][:, cut:])
-            elif q == 2:
-                nc.scalar.copy(*low)
-                nc.scalar.copy(*high)
-            else:
-                nc.vector.tensor_copy(*high)
-                cut = EXTRA_COLUMNS.get(q, 0)
-                if cut:
-                    nc.vector.tensor_copy(low[0][:, :cut], low[1][:, :cut])
-                nc.scalar.copy(low[0][:, cut:], low[1][:, cut:])
-            w1_pairs[q] = pairs
+            elif q in PAIRED:
+                nc.vector.tensor_copy(dst[:, :, :, PAIR:], src[:, :, :, PAIR:])
+                nc.vector.tensor_copy(dst[:, :EXTRA, :, :PAIR], src[:, :EXTRA, :, :PAIR])
+                nc.scalar.copy(dst[:, EXTRA:, :, :PAIR], src[:, EXTRA:, :, :PAIR])
+            elif cut:
+                nc.vector.tensor_copy(dst[:, :cut], src[:, :cut])
+            if q not in PAIRED:
+                nc.scalar.copy(dst[:, cut:], src[:, cut:])
+            w1_pairs[q] = grouped
 
         for q in range(LAST):
             if q == LOADS[load_of[q]][0]:
                 for piece in LOADS[load_of[q]]:
                     interleave(piece)
-            pairs = w1_pairs[q]
             new_codes(q)
-            quantise(q, pairs[1], PAIR, PAIR)
-            quantise(q, pairs[0], 0, PAIR)
+            for tiles in (slice(PAIR, TILES), slice(0, PAIR)) if q in PAIRED else (slice(0, TILES),):
+                cols = slice(tiles.start * P, tiles.stop * P)
+                nc.vector.quantize_mx(
+                    out=w1_codes[q][:, cols].bitcast(FP8X4),
+                    scales=w1_scales[q][:, cols],
+                    in_=w1_pairs[q][:, tiles].rearrange("p t m j -> p (t m j)"),
+                )
             first_layer_pass(q, [[2, 3, 0, 1]] * 2)
             for e in range(E - 1):
                 if q == GELU_OVER[e]:

@@ -57,7 +57,7 @@ def tile_routed_moe_kernel(tc, xT, w1, w2, gate, offs, pos1, pos2, out):
         offs_list = keep.tile([P, SLOTS // LIST_ROWS], U16, name="offs_list")
         pos1_list = keep.tile([P, T // LIST_ROWS], U16, name="pos1_list")
         pos2_list = keep.tile([P, T // LIST_ROWS], U16, name="pos2_list")
-        gate_rows = keep.tile([P, 2, T], F32, name="gate_rows")
+        gate_rows = keep.tile([P, 2, T], F32, name="gate_rows", align_bytes=256)
 
         warm = keep.tile([P, 2], F32, name="warm")
         nc.gpsimd.memset(warm[:, :1], 0.0)
@@ -69,7 +69,7 @@ def tile_routed_moe_kernel(tc, xT, w1, w2, gate, offs, pos1, pos2, out):
         nc.gpsimd.memset(token_scales[:].bitcast(I32), 0)
 
         def placed(name, shape, dtype, offset):
-            return arena.tile(shape, dtype, name=name, offset=offset, align_bytes=64)
+            return arena.tile(shape, dtype, name=name, offset=offset, align_bytes=256)
 
         x_grouped_place = [PASSES * PIECE_BYTES, PASSES * PIECE_BYTES, PIECE_BYTES]
         load_place = []
@@ -322,7 +322,7 @@ def tile_routed_moe_kernel(tc, xT, w1, w2, gate, offs, pos1, pos2, out):
         second = keep.tile([P, T], F32, name="second")
         for tokens in halves:
             nc.vector.tensor_tensor(second[:, tokens], picked[:, tokens], gate_rows[:, 1, tokens], MULT)
-        total = keep.tile([P, T], F32, name="total")
+        total = keep.tile([P, T], F32, name="total", align_bytes=256)
         for tokens in halves:
             nc.vector.tensor_tensor(total[:, tokens], first[:, tokens], second[:, tokens], ADD)
             nc.sync.dma_start(out[:, tokens], total[:, tokens])

@@ -39,7 +39,8 @@ LOADS = [[0, 1], [2, 3], [4], [5], [6], [7], [8], [9], [10]]
 LAST = PIECES - 1
 W2_BYTES = PACK * N * 4
 GELU_OVER = [5, 7, 9]
-VECTOR_COLUMNS = {2: 32, 3: 80, 4: 64, 5: 56, 6: 96, 7: 56, 8: 96, 9: 84}
+CODES_OVER = [7, 9, 10]
+VECTOR_COLUMNS = {2: 32, 3: 80, 4: 48, 5: 64, 6: 96, 7: 72, 8: 96, 9: 84}
 PAIRED = [10]
 EXTRA = 32
 VECTOR_TOKENS = [320, 64, 0]
@@ -257,8 +258,8 @@ def tile_routed_moe_kernel(tc, xT, w1, w2, gate, offs, pos1, pos2, out):
                     for b in range(2):
                         gelu(e, b, h[:, b * HALF * PACK : (b + 1) * HALF * PACK])
                     hidden_values[e] = h
-                if q == GELU_OVER[e] + 1:
-                    hidden[e] = quantise_whole(f"h{e}", hidden_values[e][:], C, load_place[load_of[q]])
+                if q == CODES_OVER[e]:
+                    hidden[e] = quantise_whole(f"h{e}", hidden_values[e][:], C, load_place[load_of[q]] + PAIR_BYTES)
 
         pairs = [placed(f"last_pair{pair}", [P, PAIR, P, PACK], BF16, pair_place(LAST, pair)) for pair in range(2)]
         for half in range(2):

@@ -195,12 +195,11 @@ def tile_routed_moe_kernel(tc, xT, w1, w2, gate, offs, pos1, pos2, out):
             return codes, scales
 
         def second_layer(sums, e, hidden):
-            codes, scales = w2_quantised[e // 2]
-            channels = slice(e % 2 * N, (e % 2 + 1) * N)
+            codes, scales = w2_quantised[e]
             nc.tensor.matmul_mx(
                 out=sums,
-                lhsT=codes[:, channels].bitcast(FP8X4),
-                lhsT_scale=scales[:, channels],
+                lhsT=codes.bitcast(FP8X4),
+                lhsT_scale=scales,
                 rhs=hidden[0][:].bitcast(FP8X4),
                 rhs_scale=hidden[1][:],
                 start=True,
@@ -279,8 +278,13 @@ def tile_routed_moe_kernel(tc, xT, w1, w2, gate, offs, pos1, pos2, out):
         def interleave_w2(e, copy):
             copy(*by_lines(w2_grouped[e // 2][:, e % 2], w2_raw[e][:]))
 
-        def quantise_w2(pair):
-            return quantise_whole(f"w2_{pair}", w2_grouped[pair][:].rearrange("p e n j -> p (e n j)"), 2 * N)
+        def quantise_w2(first, experts):
+            values = w2_grouped[first // 2][:, first % 2 : first % 2 + experts].rearrange("p e n j -> p (e n j)")
+            codes, scales = quantise_whole(f"w2_{first}", values, experts * N)
+            for n in range(experts):
+                w2_quantised[first + n] = (codes[:, n * N : (n + 1) * N], scales[:, n * N : (n + 1) * N])
+
+        w2_quantised = {}
 
         interleave_w2(0, nc.scalar.copy)
         last_h = []
@@ -289,10 +293,10 @@ def tile_routed_moe_kernel(tc, xT, w1, w2, gate, offs, pos1, pos2, out):
             gelu(E - 1, b, h[:])
             last_h.append(h)
         interleave_w2(1, nc.vector.tensor_copy)
-        w2_quantised = [quantise_w2(0)]
-        interleave_w2(2, nc.vector.tensor_copy)
-        interleave_w2(3, nc.vector.tensor_copy)
-        w2_quantised.append(quantise_w2(1))
+        quantise_w2(0, 2)
+        for e in range(2, E):
+            interleave_w2(e, nc.vector.tensor_copy)
+            quantise_w2(e, 1)
         last_hidden = []
         for b in range(2):
             last_hidden.append(quantise_whole(f"h_last{b}", last_h[b][:], HALF, w2_place[-1] + b * HALF * 4))

@@ -41,6 +41,7 @@ W2_BYTES = PACK * N * 4
 GELU_OVER = [5, 7, 9]
 CODES_OVER = [7, 9, 10]
 VECTOR_COLUMNS = {2: 32, 3: 80, 4: 48, 5: 64, 6: 96, 7: 72, 8: 96, 9: 84}
+LAST_PARTS = [(0, 128), (128, 192), (192, 256)]
 PAIRED = [10]
 EXTRA = 32
 VECTOR_TOKENS = [320, 64, 0]
@@ -180,10 +181,9 @@ def tile_routed_moe_kernel(tc, xT, w1, w2, gate, offs, pos1, pos2, out):
                         stop=(g == PASSES - 1 and n == TILES - 1),
                     )
 
-        def gelu(e, b, h):
-            nc.scalar.activation(
-                h.rearrange("p (s t) -> p s t", t=TILES), hidden_sums[(e, b)][:].rearrange("p t s -> p s t"), GELU
-            )
+        def gelu(e, b, h, slots=slice(0, HALF)):
+            sums = hidden_sums[(e, b)][:, :, slots].rearrange("p t s -> p s t")
+            nc.scalar.activation(h.rearrange("p (s t) -> p s t", t=TILES), sums, GELU)
 
         def quantise_whole(name, values, columns, place=None):
             if place is None:
@@ -271,7 +271,7 @@ def tile_routed_moe_kernel(tc, xT, w1, w2, gate, offs, pos1, pos2, out):
         first_layer_pass(LAST, [tile_order, tile_order[::-1]])
 
         w2_grouped = []
-        for pair, place in enumerate([last_place[1], pair_place(LAST, 0)]):
+        for pair, place in enumerate([last_place[0], pair_place(LAST, 0)]):
             grouped = placed(f"w2_grouped{pair}", [P, 2, N, PACK], BF16, place)
             w2_grouped.append(grouped)
 
@@ -288,34 +288,36 @@ def tile_routed_moe_kernel(tc, xT, w1, w2, gate, offs, pos1, pos2, out):
 
         interleave_w2(0, nc.scalar.copy)
         last_h = []
-        for b in range(2):
-            h = placed(f"h_last{b}", [P, HALF * PACK], BF16, w2_place[0] + b * HALF * PACK * 2)
-            gelu(E - 1, b, h[:])
+        for first, end in LAST_PARTS:
+            h = placed(f"h_last{first}", [P, (end - first) * PACK], BF16, w2_place[0] + first * PACK * 2)
+            gelu(E - 1, first // HALF, h[:], slice(first % HALF, first % HALF + end - first))
             last_h.append(h)
         interleave_w2(1, nc.vector.tensor_copy)
         quantise_w2(0, 2)
         for e in range(2, E):
             interleave_w2(e, nc.vector.tensor_copy)
-            quantise_w2(e, 1)
         last_hidden = []
-        for b in range(2):
-            last_hidden.append(quantise_whole(f"h_last{b}", last_h[b][:], HALF, w2_place[-1] + b * HALF * 4))
+        for b, (first, end) in enumerate(LAST_PARTS):
+            if b < 2:
+                quantise_w2(2 + b, 1)
+            place = w2_place[2 + first // HALF] + first % HALF * 4
+            last_hidden.append(quantise_whole(f"h_last{first}", last_h[b][:], end - first, place))
 
         y_slots = keep.tile([P, SLOTS], F32, name="y_slots")
-        y_first = psum_y.tile([P, 2 * C], F32, name="y_first")
+        y_first = psum_h.tile([P, 2 * C], F32, name="hidden_sums")
         for e in range(2):
             second_layer(y_first[:, e * C : (e + 1) * C], e, hidden[e])
         y_third = psum_y.tile([P, C], F32, name="y_third")
         second_layer(y_third[:], 2, hidden[2])
         y_last = []
-        for b in range(2):
-            sums = psum_y.tile([P, HALF], F32, name=f"y_last{b}")
-            second_layer(sums[:], 3, last_hidden[b])
+        for moving, (first, end) in zip(last_hidden, LAST_PARTS):
+            sums = psum_y.tile([P, end - first], F32, name=f"y_last{first}")
+            second_layer(sums[:], 3, moving)
             y_last.append(sums)
         nc.scalar.copy(y_slots[:, : 2 * C], y_first[:])
         nc.scalar.copy(y_slots[:, 2 * C : 3 * C], y_third[:])
-        nc.scalar.copy(y_slots[:, 3 * C : 3 * C + HALF], y_last[0][:])
-        nc.vector.tensor_copy(y_slots[:, 3 * C + HALF :], y_last[1][:])
+        for copy, sums, (first, end) in zip([nc.scalar.copy, nc.vector.tensor_copy, nc.vector.tensor_copy], y_last, LAST_PARTS):
+            copy(y_slots[:, 3 * C + first : 3 * C + end], sums[:])
 
         halves = [slice(0, T // 2), slice(T // 2, T)]
         first = keep.tile([P, T], F32, name="first")

from contextlib import ExitStack

import concourse.mybir as mybir

K, T, E, C, H, N = 1536, 512, 4, 256, 512, 128
FLOPS = 2 * E * C * H * (K + N)

F32 = mybir.dt.float32
BF16 = mybir.dt.bfloat16
I32 = mybir.dt.int32
U32 = mybir.dt.uint32
U16 = mybir.dt.uint16
U8 = mybir.dt.uint8
FP8X4 = mybir.dt.float8_e4m3fn_x4

MULT = mybir.AluOpType.mult
ADD = mybir.AluOpType.add
GELU = mybir.ActivationFunctionType.Gelu_apprx_tanh

P = 128
PACK = 4
K_PASS = P * PACK
PASSES = K // K_PASS
PIECES = E * PASSES
SLOTS = E * C
HALF = C // 2
TILES = H // P
LINE = 4
LIST_ROWS = 16

SCALE_ROWS = 4
WINDOW = 1408
COPY = mybir.ActivationFunctionType.Copy

PAIR = 2
PIECE_BYTES = PACK * H * 4
PAIR_BYTES = PAIR * P * PACK * 2
LOADS = [[0, 1], [2, 3], [4], [5], [6], [7], [8], [9], [10]]
LAST = PIECES - 1
W2_BYTES = PACK * N * 4
GELU_OVER = [5, 7, 9]
CODES_OVER = [7, 9, 10]
VECTOR_COLUMNS = {2: 32, 3: 80, 4: 48, 5: 64, 6: 96, 7: 72, 8: 96, 9: 84}
LAST_PARTS = [(0, 128), (128, 192), (192, 256)]
PAIRED = [10]
EXTRA = 32
VECTOR_TOKENS = [320, 64, 0]
GPSIMD_COLUMNS = 48


def tile_routed_moe_kernel(tc, xT, w1, w2, gate, offs, pos1, pos2, out):
    nc = tc.nc
    with ExitStack() as ctx:
        keep = ctx.enter_context(tc.tile_pool(name="keep", bufs=1))
        arena = ctx.enter_context(tc.tile_pool(name="arena", bufs=1))
        psum_h = ctx.enter_context(tc.psum_pool(name="psum_h", bufs=4))
        psum_y = ctx.enter_context(tc.psum_pool(name="psum_y", bufs=1))

        offs_list = keep.tile([P, SLOTS // LIST_ROWS], U16, name="offs_list")
        pos1_list = keep.tile([P, T // LIST_ROWS], U16, name="pos1_list")
        pos2_list = keep.tile([P, T // LIST_ROWS], U16, name="pos2_list")
        gate_rows = keep.tile([P, 2, T], F32, name="gate_rows", align_bytes=256)

        warm = keep.tile([P, 2], F32, name="warm")
        nc.gpsimd.memset(warm[:, :1], 0.0)
        nc.scalar.activation(warm[:, 1:], warm[:, :1], GELU)

        token_codes = keep.tile([P, PASSES, WINDOW], U32, name="token_codes", align_bytes=64)
        nc.gpsimd.memset(token_codes[:, :, T:].bitcast(I32), 0)
        token_scales = keep.tile([P, WINDOW], U8, name="token_scales", align_bytes=64)
        nc.gpsimd.memset(token_scales[:].bitcast(I32), 0)

        def placed(name, shape, dtype, offset):
            return arena.tile(shape, dtype, name=name, offset=offset, align_bytes=256)

        x_grouped_place = [PASSES * PIECE_BYTES, PASSES * PIECE_BYTES, PIECE_BYTES]
        load_place = []
        place = PASSES * PIECE_BYTES + 2 * PAIR_BYTES
        for pieces in LOADS:
            load_place.append(place)
            place += len(pieces) * PIECE_BYTES + PAIR_BYTES
        last_place = [place, place + PIECE_BYTES // 2]
        w2_place = [place + PIECE_BYTES + e * W2_BYTES for e in range(E)]
        load_of = {q: i for i, pieces in enumerate(LOADS) for q in pieces}
        load_of[LAST] = len(LOADS)

        x_raw = []
        for g in range(PASSES):
            raw = placed(f"x_raw{g}", [P, PACK, T], F32, g * PIECE_BYTES)
            nc.sync.dma_start(raw[:], xT[g * K_PASS : (g + 1) * K_PASS, :].rearrange("(p j) t -> p j t", j=PACK))
            x_raw.append(raw)
            if g == 0:
                nc.sync.dma_start(offs_list[:], offs)
        w1_rows = w1.rearrange("e (g p j) c -> p (e g) j c", p=P, j=PACK)
        w1_raw = {}
        for i, pieces in enumerate(LOADS):
            raw = placed(f"w1_raw{i}", [P, len(pieces), PACK, H], F32, load_place[i])
            nc.sync.dma_start(raw[:], w1_rows[:, pieces[0] : pieces[-1] + 1])
            for n, q in enumerate(pieces):
                w1_raw[q] = raw[:, n]
        last_raw = []
        for half in range(2):
            raw = placed(f"last_raw{half}", [P, PACK, H // 2], F32, last_place[half])
            nc.sync.dma_start(raw[:], w1_rows[:, LAST, :, half * (H // 2) : (half + 1) * (H // 2)])
            last_raw.append(raw)
        w2_rows = w2.rearrange("e (p j) n -> p e j n", j=PACK)
        w2_raw = []
        for e in range(E):
            raw = placed(f"w2_raw{e}", [P, PACK, N], F32, w2_place[e])
            nc.sync.dma_start(raw[:], w2_rows[:, e])
            w2_raw.append(raw)
        nc.sync.dma_start(pos1_list[:], pos1)
        nc.sync.dma_start(pos2_list[:], pos2)
        nc.sync.dma_start(gate_rows[:], gate.rearrange("r n t -> n r t"))

        def by_lines(dst, src):
            return dst.rearrange("p (c i) j -> p c j i", i=LINE), src.rearrange("p j (c i) -> p c j i", i=LINE)

        slot_codes = []
        slot_scales = keep.tile([P, SLOTS], U8, name="slot_scales", align_bytes=64)
        for g in range(PASSES):
            grouped = placed(f"x_grouped{g}", [P, T, PACK], BF16, x_grouped_place[g])
            cut = VECTOR_TOKENS[g]
            if cut:
                nc.vector.tensor_copy(*by_lines(grouped[:, :cut], x_raw[g][:, :, :cut]))
            middle = (cut + T) // 2
            for part in (slice(cut, middle), slice(middle, T)):
                nc.scalar.copy(*by_lines(grouped[:, part], x_raw[g][:, :, part]))
            nc.vector.quantize_mx(
                out=token_codes[:, g, :T].bitcast(FP8X4),
                scales=token_scales[SCALE_ROWS * g : P, :T],
                in_=grouped[:].rearrange("p t j -> p (t j)"),
            )
            if g == PASSES - 1:
                nc.vector.tensor_copy(slot_scales[:], token_scales[:].indirect(offs_list[:]))
            codes = keep.tile([P, SLOTS], U32, name=f"slot_codes{g}", align_bytes=64)
            nc.vector.tensor_copy(codes[:], token_codes[:, g, :].indirect(offs_list[:]))
            slot_codes.append(codes)

        def pair_views(grouped, raw, pair, first):
            src = raw.rearrange("p j (m t) -> p m j t", t=TILES)[:, :, :, PAIR * pair : PAIR * (pair + 1)]
            dst = grouped[:].rearrange("p t m j -> p m j t")[:, first : first + src.shape[1]]
            return dst, src

        def pair_place(q, pair):
            return load_place[-1 - pair] + 2 * PAIR_BYTES

        w1_codes = {}
        w1_scales = {}

        def new_codes(q):
            w1_codes[q] = keep.tile([P, H], U32, name=f"w1_codes{q}", align_bytes=64)
            w1_scales[q] = keep.tile([P, H], U8, name=f"w1_scales{q}", align_bytes=64)

        def quantise(q, grouped, first_tile, tiles):
            cols = slice(first_tile * P, (first_tile + tiles) * P)
            part = grouped[:, first_tile % PAIR : first_tile % PAIR + tiles]
            nc.vector.quantize_mx(
                out=w1_codes[q][:, cols].bitcast(FP8X4),
                scales=w1_scales[q][:, cols],
                in_=part.rearrange("p t m j -> p (t m j)"),
            )

        hidden_sums = {}

        def first_layer_pass(q, orders):
            e, g = q // PASSES, q % PASSES
            for b in range(2):
                if g == 0:
                    hidden_sums[(e, b)] = psum_h.tile([P, TILES, HALF], F32, name="hidden_sums")
                cols = slice(e * C + b * HALF, e * C + (b + 1) * HALF)
                for n, t in enumerate(orders[b]):
                    channels = slice(t * P, (t + 1) * P)
                    nc.tensor.matmul_mx(
                        out=hidden_sums[(e, b)][:, t, :],
                        lhsT=w1_codes[q][:, channels].bitcast(FP8X4),
                        lhsT_scale=w1_scales[q][:, channels],
                        rhs=slot_codes[g][:, cols].bitcast(FP8X4),
                        rhs_scale=slot_scales[SCALE_ROWS * g : P, cols],
                        start=(g == 0 and n == 0),
                        stop=(g == PASSES - 1 and n == TILES - 1),
                    )

        def gelu(e, b, h, slots=slice(0, HALF)):
            sums = hidden_sums[(e, b)][:, :, slots].rearrange("p t s -> p s t")
            nc.scalar.activation(h.rearrange("p (s t) -> p s t", t=TILES), sums, GELU)

        def quantise_whole(name, values, columns, place=None):
            if place is None:
                codes = keep.tile([P, columns], U32, name=name + "_codes", align_bytes=64)
            else:
                codes = placed(name + "_codes", [P, columns], U32, place)
            scales = keep.tile([P, columns], U8, name=name + "_scales", align_bytes=64)
            nc.vector.quantize_mx(out=codes[:].bitcast(FP8X4), scales=scales[:], in_=values)
            return codes, scales

        def second_layer(sums, e, hidden):
            codes, scales = w2_quantised[e]
            nc.tensor.matmul_mx(
                out=sums,
                lhsT=codes.bitcast(FP8X4),
                lhsT_scale=scales,
                rhs=hidden[0][:].bitcast(FP8X4),
                rhs_scale=hidden[1][:],
                start=True,
                stop=True,
            )

        hidden = {}
        hidden_values = {}
        w1_pairs = {}

        def piece_place(q):
            i = load_of[q]
            if i == 0:
                return x_grouped_place[-1] + q * 2 * PAIR_BYTES
            if i == 1:
                return (q - LOADS[i][0]) * 2 * PAIR_BYTES
            return load_place[i - 1] + (q - LOADS[i][0] + 1) * 2 * PAIR_BYTES

        def interleave(q):
            grouped = placed(f"w1_grouped{q}", [P, TILES, P, PACK], BF16, piece_place(q))
            dst = grouped[:].rearrange("p t m j -> p m j t")
            src = w1_raw[q].rearrange("p j (m t) -> p m j t", t=TILES)
            cut = GPSIMD_COLUMNS if load_of[q] == 0 else VECTOR_COLUMNS.get(q, 0)
            if load_of[q] == 0:
                order = "p m j t -> p t m j"
                nc.gpsimd.tensor_scalar(
                    dst[:, :cut].rearrange(order), src[:, :cut].rearrange(order), 1.0, 0.0, MULT, ADD
                )
            elif q in PAIRED:
                nc.vector.tensor_copy(dst[:, :, :, PAIR:], src[:, :, :, PAIR:])
                nc.vector.tensor_copy(dst[:, :EXTRA, :, :PAIR], src[:, :EXTRA, :, :PAIR])
                nc.scalar.copy(dst[:, EXTRA:, :, :PAIR], src[:, EXTRA:, :, :PAIR])
            elif cut:
                nc.vector.tensor_copy(dst[:, :cut], src[:, :cut])
            if q not in PAIRED:
                nc.scalar.copy(dst[:, cut:], src[:, cut:])
            w1_pairs[q] = grouped

        for q in range(LAST):
            if q == LOADS[load_of[q]][0]:
                for piece in LOADS[load_of[q]]:
                    interleave(piece)
            new_codes(q)
            for tiles in (slice(PAIR, TILES), slice(0, PAIR)) if q in PAIRED else (slice(0, TILES),):
                cols = slice(tiles.start * P, tiles.stop * P)
                nc.vector.quantize_mx(
                    out=w1_codes[q][:, cols].bitcast(FP8X4),
                    scales=w1_scales[q][:, cols],
                    in_=w1_pairs[q][:, tiles].rearrange("p t m j -> p (t m j)"),
                )
            first_layer_pass(q, [[2, 3, 0, 1]] * 2)
            for e in range(E - 1):
                if q == GELU_OVER[e]:
                    h = placed(f"h{e}", [P, C * PACK], BF16, load_place[load_of[q]])
                    for b in range(2):
                        gelu(e, b, h[:, b * HALF * PACK : (b + 1) * HALF * PACK])
                    hidden_values[e] = h
                if q == CODES_OVER[e]:
                    hidden[e] = quantise_whole(f"h{e}", hidden_values[e][:], C, load_place[load_of[q]] + PAIR_BYTES)

        pairs = [placed(f"last_pair{pair}", [P, PAIR, P, PACK], BF16, pair_place(LAST, pair)) for pair in range(2)]
        for half in range(2):
            nc.vector.tensor_copy(*pair_views(pairs[1], last_raw[half][:], 1, half * P // 2))
            nc.scalar.copy(*pair_views(pairs[0], last_raw[half][:], 0, half * P // 2))
        new_codes(LAST)
        tile_order = [2, 3, 0, 1]
        for t in tile_order:
            quantise(LAST, pairs[t // PAIR], t, 1)
        first_layer_pass(LAST, [tile_order, tile_order[::-1]])

        w2_grouped = []
        for pair, place in enumerate([last_place[0], pair_place(LAST, 0)]):
            grouped = placed(f"w2_grouped{pair}", [P, 2, N, PACK], BF16, place)
            w2_grouped.append(grouped)

        def interleave_w2(e, copy):
            copy(*by_lines(w2_grouped[e // 2][:, e % 2], w2_raw[e][:]))

        def quantise_w2(first, experts):
            values = w2_grouped[first // 2][:, first % 2 : first % 2 + experts].rearrange("p e n j -> p (e n j)")
            codes, scales = quantise_whole(f"w2_{first}", values, experts * N)
            for n in range(experts):
                w2_quantised[first + n] = (codes[:, n * N : (n + 1) * N], scales[:, n * N : (n + 1) * N])

        w2_quantised = {}

        interleave_w2(0, nc.scalar.copy)
        last_h = []
        for first, end in LAST_PARTS:
            h = placed(f"h_last{first}", [P, (end - first) * PACK], BF16, w2_place[0] + first * PACK * 2)
            gelu(E - 1, first // HALF, h[:], slice(first % HALF, first % HALF + end - first))
            last_h.append(h)
        interleave_w2(1, nc.vector.tensor_copy)
        quantise_w2(0, 2)
        for e in range(2, E):
            interleave_w2(e, nc.vector.tensor_copy)
        last_hidden = []
        for b, (first, end) in enumerate(LAST_PARTS):
            if b < 2:
                quantise_w2(2 + b, 1)
            place = w2_place[2 + first // HALF] + first % HALF * 4
            last_hidden.append(quantise_whole(f"h_last{first}", last_h[b][:], end - first, place))

        y_slots = keep.tile([P, SLOTS], F32, name="y_slots")
        y_first = psum_h.tile([P, 2 * C], F32, name="hidden_sums")
        for e in range(2):
            second_layer(y_first[:, e * C : (e + 1) * C], e, hidden[e])
        y_third = psum_y.tile([P, C], F32, name="y_third")
        second_layer(y_third[:], 2, hidden[2])
        y_last = []
        for moving, (first, end) in zip(last_hidden, LAST_PARTS):
            sums = psum_y.tile([P, end - first], F32, name=f"y_last{first}")
            second_layer(sums[:], 3, moving)
            y_last.append(sums)
        nc.scalar.copy(y_slots[:, : 2 * C], y_first[:])
        nc.scalar.copy(y_slots[:, 2 * C : 3 * C], y_third[:])
        for copy, sums, (first, end) in zip([nc.scalar.copy, nc.vector.tensor_copy, nc.vector.tensor_copy], y_last, LAST_PARTS):
            copy(y_slots[:, 3 * C + first : 3 * C + end], sums[:])

        halves = [slice(0, T // 2), slice(T // 2, T)]
        first = keep.tile([P, T], F32, name="first")
        nc.vector.tensor_tensor(first[:], y_slots[:].indirect(pos1_list[:]), gate_rows[:, 0, :], MULT)
        picked = keep.tile([P, T], F32, name="picked")
        for tokens in halves:
            entries = pos2_list[:, tokens.start // LIST_ROWS : tokens.stop // LIST_ROWS]
            nc.scalar.activation(picked[:, tokens], y_slots[:].indirect(entries), COPY)
        second = keep.tile([P, T], F32, name="second")
        for tokens in halves:
            nc.vector.tensor_tensor(second[:, tokens], picked[:, tokens], gate_rows[:, 1, tokens], MULT)
        total = keep.tile([P, T], F32, name="total", align_bytes=256)
        for tokens in halves:
            nc.vector.tensor_tensor(total[:, tokens], first[:, tokens], second[:, tokens], ADD)
            nc.sync.dma_start(out[:, tokens], total[:, tokens])
